import numpy as np
import ml_dtypes


def mxq(x, axis, fmt="e4m3"):
    dtype, down = {"e4m3": (ml_dtypes.float8_e4m3fn, 7), "e5m2": (ml_dtypes.float8_e5m2, 14)}[fmt]
    v = np.moveaxis(np.asarray(x, np.float32).astype(ml_dtypes.bfloat16).astype(np.float64), axis, -1)
    blocks = v.reshape(v.shape[:-1] + (-1, 32))
    amax = np.abs(blocks).max(-1, keepdims=True)
    byte = np.maximum(np.where(amax > 0, np.frexp(amax)[1] - 1 + 127, 0) - down, 1)
    scale = np.exp2(byte - 127.0)
    codes = (blocks / scale).astype(np.float32).astype(dtype).astype(np.float64)
    return np.moveaxis((codes * scale).reshape(v.shape), -1, axis)


WIDE = False


def mx_kscale(k):
    if not WIDE:
        return np.ones(k)
    levels = np.array([10, -10, 5, -5, 0])
    if k % 512:
        return np.exp2(np.random.permutation(np.resize(levels, k // 32))).repeat(32)
    a = np.empty((k // 512, 16))
    for p in range(k // 512):
        a[p, :8] = np.random.permutation(np.resize(levels, 8))
        for g in range(8):
            far = levels[np.abs(levels - a[p, g]) >= 10]
            a[p, g + 8] = far[np.random.randint(len(far))]
    return np.exp2(a.ravel()).repeat(32)


BF16 = ml_dtypes.bfloat16


def bf(x):
    return np.asarray(x, np.float32).astype(BF16)


def f64(x):
    return np.asarray(x).astype(np.float64)


H, TQ, TK, E, DV, M = 2, 1024, 1024, 512, 512, 3


def coef_draw():
    sign = np.where(np.random.uniform(0.0, 1.0, (H, M)) < 0.5, -1.0, 1.0)
    return sign * np.random.uniform(0.4, 1.0, (H, M))


def draw0():
    s, t = mx_kscale(E), mx_kscale(TK)
    return {
        "q": bf(np.random.standard_normal((H, TQ, E)) * s),
        "k": bf(np.random.standard_normal((H, TK, E)) / s),
        "v": bf(np.random.standard_normal((H, TK, DV)) / t[:, None]),
        "ca": bf(coef_draw()),
        "cb": bf(coef_draw()),
        "g": bf((1.0 + 0.1 * np.random.standard_normal((H, TK))) * t),
    }


def fourier_map(s, ca, cb):
    a = np.zeros_like(s)
    for i in range(ca.shape[1]):
        ms = float(i + 1) * s
        cos_coef = ca[:, i][:, None, None]
        sin_coef = cb[:, i][:, None, None]
        a = a + (cos_coef * np.cos(ms) + sin_coef * np.sin(ms))
    return a


def core(q, k, v, ca, cb, g):
    t = k.shape[1]
    e = q.shape[2]
    qq = mxq(f64(q), 2, "e4m3")
    kq = mxq(f64(k), 2, "e4m3")
    s = (qq @ kq.transpose(0, 2, 1)) / np.sqrt(e)
    a = fourier_map(s, f64(ca), f64(cb))
    ag = a * f64(g)[:, None, :]
    return (mxq(ag, 2, "e4m3") @ mxq(f64(v), 1, "e4m3")) / np.sqrt(t)


def e4m3fn_bytes(y):
    return np.clip(np.asarray(y, np.float64), -448.0, 448.0).astype(np.float32).astype(ml_dtypes.float8_e4m3fn).view(np.uint8)


def e4m3fn_values(b):
    return np.asarray(b, np.uint8).view(ml_dtypes.float8_e4m3fn).astype(np.float64)


def setup_inputs():
    d = draw0()
    x0 = np.asarray(d['v']).astype(np.float64)
    s = (np.max(np.abs(x0), axis=(0, 2), keepdims=True) / 448.0).astype(np.float32)
    out = {}
    for k, v in d.items():
        if k == 'v':
            out['v_bytes'] = e4m3fn_bytes(x0 / s.astype(np.float64))
            out['v_scale'] = s
        else:
            out[k] = v
    return out


def reference(q, k, v_bytes, v_scale, ca, cb, g):
    return core(q, k, e4m3fn_values(v_bytes) * v_scale.astype(np.float64), ca, cb, g)

@@ -1,0 +1,435 @@
+import math
+from contextlib import ExitStack
+
+import concourse.mybir as mybir
+from concourse.masks import make_identity
+
+H, TQ, TK, E, DV, HARMONICS = 2, 1024, 1024, 512, 512, 3
+FLOPS = 2 * H * TQ * TK * E + 2 * H * TQ * TK * DV
+
+F32 = mybir.dt.float32
+BF16 = mybir.dt.bfloat16
+I32 = mybir.dt.int32
+U32 = mybir.dt.uint32
+U8 = mybir.dt.uint8
+FP8 = mybir.dt.float8_e4m3fn
+FP8X4 = mybir.dt.float8_e4m3fn_x4
+ALU = mybir.AluOpType
+ACT = mybir.ActivationFunctionType
+AXIS_X = mybir.AxisListType.X
+
+P = 128
+PACK = 4
+K_PASS = P * PACK
+PASSES = TK // K_PASS
+Q_TILES = TQ // P
+TILES = H * Q_TILES
+NEWTON_STEPS = 2
+WHOLE_ON_POOL = True
+FLOOR = 2.0 ** -60
+BANKS = {"score": 4, "sum": 2, "out": 1, "turn": 1}
+
+
+def tile_fourierkolmogorovarnoldattention_kernel(tc, q, k, v_bytes, v_scale, ca, cb, g, out):
+    nc = tc.nc
+    vec, act, pe, pool_engine, dma = nc.vector, nc.scalar, nc.tensor, nc.gpsimd, nc.sync
+
+    with ExitStack() as ctx:
+        keep = ctx.enter_context(tc.tile_pool(name="keep", bufs=1))
+        work = ctx.enter_context(tc.tile_pool(name="work", bufs=2))
+        psum = ctx.enter_context(tc.psum_pool(name="psum", bufs=2))
+        ctx.enter_context(tc.manual_schedule())
+
+        def kept(name, shape, dtype):
+            return keep.tile(shape, dtype, name=name, align_bytes=64)
+
+        ca_sb = kept("ca_sb", [P, H * HARMONICS], BF16)
+        cb_sb = kept("cb_sb", [P, H * HARMONICS], BF16)
+        k_rows = [[kept("k_rows%d%d" % (h, j), [P, 2 * E], BF16) for j in range(2 * PASSES)] for h in range(H)]
+        q_rows = [kept("q_rows%d" % j, [P, 2 * E], BF16) for j in range(TILES // 2)]
+        v_raw = [[kept("v_raw%d%d" % (h, c), [P, PACK * DV], U8) for c in range(PASSES)] for h in range(H)]
+        v_scale_sb = kept("v_scale_sb", [P, PASSES, PACK], F32)
+        gain_sb = kept("gain_sb", [P, H * PASSES, PACK], BF16)
+
+        def load_k(h, j):
+            c, half = divmod(j, 2)
+            rows = k[h, c * K_PASS:(c + 1) * K_PASS, :].rearrange("(m t) e -> m (t e)", t=PACK)
+            dma.dma_start(out=k_rows[h][j][:], in_=rows[:, half * 2 * E:(half + 1) * 2 * E])
+
+        def load_q(j):
+            h, first = divmod(2 * j, Q_TILES)
+            dma.dma_start(out=q_rows[j][:].rearrange("p (i e) -> p i e", i=2),
+                          in_=q[h, first * P:(first + 2) * P, :].rearrange("(i p) e -> p i e", p=P))
+
+        def load_v(h, c):
+            dma.dma_start(out=v_raw[h][c][:], in_=v_bytes[h, c * K_PASS:(c + 1) * K_PASS, :].rearrange("(p t) n -> p (t n)", t=PACK))
+
+        act.dma_start(out=ca_sb[:], in_=ca.rearrange("h m -> (h m)").partition_broadcast(P))
+        act.dma_start(out=cb_sb[:], in_=cb.rearrange("h m -> (h m)").partition_broadcast(P))
+        load_k(0, 0)
+        load_q(0)
+        for j in range(1, 2 * PASSES):
+            load_k(0, j)
+        dma.dma_start(out=v_scale_sb[:], in_=v_scale.rearrange("o (c p t) x -> p (o c) (t x)", p=P, t=PACK))
+        load_v(0, 0)
+        load_q(1)
+        load_v(0, 1)
+        dma.dma_start(out=gain_sb[:], in_=g.rearrange("h (c p t) -> p (h c) t", p=P, t=PACK))
+        load_q(2)
+        load_q(3)
+        for j in range(2 * PASSES):
+            load_k(1, j)
+        for j in range(4, TILES // 2):
+            load_q(j)
+        for c in range(PASSES):
+            load_v(1, c)
+
+        ident = kept("ident", [P, P], F32)
+        make_identity(nc, ident[:])
+        exponent = kept("exponent", [P, 2, H], F32)
+        pool_engine.memset(exponent[:, 0, :], -0.5)
+        pool_engine.memset(exponent[:, 1, :], 0.5)
+        warm = kept("warm", [P, 2], F32)
+        vec.memset(warm[:, 0:1], 0.0)
+        act.activation(out=warm[:, 1:2], in_=warm[:, 0:1], func=ACT.Sin)
+
+        k_codes = [[kept("k_codes%d%d" % (h, c), [P, K_PASS], U32) for c in range(PASSES)] for h in range(H)]
+        k_scales = [[kept("k_scales%d%d" % (h, c), [P, K_PASS], U8) for c in range(PASSES)] for h in range(H)]
+        q_codes = [kept("q_codes%d" % j, [P, 2 * P], U32) for j in range(TILES // 2)]
+        q_scales = [kept("q_scales%d" % j, [P, 2 * P], U8) for j in range(TILES // 2)]
+        v_codes = [[kept("v_codes%d%d" % (h, c), [P, DV], U32) for c in range(PASSES)] for h in range(H)]
+        v_scales = [[kept("v_scales%d%d" % (h, c), [P, DV], U8) for c in range(PASSES)] for h in range(H)]
+
+        def k_job(h, j):
+            c, half = divmod(j, 2)
+            cols = slice(half * 2 * P, (half + 1) * 2 * P)
+            return (k_rows[h][j][:], k_codes[h][c][:, cols], k_scales[h][c][:, cols])
+
+        def q_job(j):
+            return (q_rows[j][:], q_codes[j][:], q_scales[j][:])
+
+        def turn(job, tag):
+            words = job[0].bitcast(F32)
+            bank = psum.tile([P, 2, 2, P], F32, name="turn_bank", tag=tag, bufs=BANKS[tag])
+            for i in range(2):
+                for u in range(2):
+                    pe.transpose(bank[:, i, u, :], words[:, i * (E // 2) + u:(i + 1) * (E // 2):2], ident[:])
+            return bank
+
+        def turned_copy(bank, engine):
+            grouped = work.tile([P, 2 * P * PACK], BF16, name="grouped", align_bytes=64, bufs=3)
+            dst = grouped[:].bitcast(F32).rearrange("p (i r u) -> p i r u", i=2, u=2)
+            src = bank[:].rearrange("p i u r -> p i r u")
+            if engine is act:
+                act.copy(out=dst, in_=src)
+            else:
+                vec.tensor_copy(out=dst, in_=src)
+            return grouped
+
+        def quantize(codes, scales, values):
+            vec.quantize_mx(out=codes.bitcast(FP8X4), scales=scales, in_=values)
+
+        def widen_v(h, c, engine):
+            planes = work.tile([P, PACK, DV], BF16, name="v_planes", align_bytes=64)
+            for t in range(PACK):
+                src = v_raw[h][c][:, t * DV:(t + 1) * DV].bitcast(FP8)
+                if engine is act:
+                    act.activation(out=planes[:, t, :], in_=src, func=ACT.Copy, scale=v_scale_sb[:, c, t:t + 1])
+                else:
+                    vec.tensor_scalar(out=planes[:, t, :], in0=src, scalar1=v_scale_sb[:, c, t:t + 1], scalar2=None, op0=ALU.mult)
+            return planes
+
+        def interleave_v(planes, engine):
+            woven = work.tile([P, DV * PACK], BF16, name="v_woven", align_bytes=64)
+            dst = woven[:].rearrange("p (n t) -> p n t", t=PACK)
+            src = planes[:].rearrange("p t n -> p n t")
+            if engine is act:
+                act.copy(out=dst, in_=src)
+            else:
+                vec.tensor_copy(out=dst, in_=src)
+            return woven
+
+        def small(name, *shape):
+            return kept(name, [P] + list(shape), F32)
+
+        def mul(name, a, b):
+            o = small(name, H)
+            vec.tensor_tensor(out=o[:], in0=a, in1=b, op=ALU.mult)
+            return o
+
+        def fused(name, a, scalar, b, op0, op1):
+            o = small(name, H)
+            vec.scalar_tensor_tensor(out=o[:], in0=a, scalar=scalar, in1=b, op0=op0, op1=op1)
+            return o
+
+        def scaled(name, a, factor):
+            o = small(name, H)
+            vec.tensor_scalar(out=o[:], in0=a, scalar1=factor, scalar2=None, op0=ALU.mult)
+            return o
+
+        def affine(name, a, s1, s2, op0, op1):
+            o = small(name, H)
+            vec.tensor_scalar(out=o[:], in0=a, scalar1=s1, scalar2=s2, op0=op0, op1=op1)
+            return o
+
+        ba = small("ba", HARMONICS, H, 2)
+        vec.tensor_copy(out=ba[:, :, :, 0], in_=cb_sb[:].rearrange("p (h m) -> p m h", h=H))
+        vec.tensor_copy(out=ba[:, :, :, 1], in_=ca_sb[:].rearrange("p (h m) -> p m h", h=H))
+        third = ba[:, 2, :, :]
+        squares = small("squares", H, 2)
+        vec.tensor_tensor(out=squares[:], in0=third, in1=third, op=ALU.mult)
+        taxi = small("taxi", H)
+        vec.tensor_reduce(out=taxi[:], in_=third, op=ALU.add, axis=AXIS_X, apply_absolute_value=True)
+        radius2 = fused("radius2", squares[:, :, 0], FLOOR * FLOOR, squares[:, :, 1], ALU.add, ALU.add)
+        inv_radius = small("inv_radius", H)
+        pool_engine.tensor_tensor(out=inv_radius[:], in0=radius2[:], in1=exponent[:, 0, :], op=ALU.pow)
+        taxi_safe = affine("taxi_safe", taxi[:], FLOOR, 1.0 / math.pi, ALU.add, ALU.mult)
+        half_sign3 = affine("half_sign3", third[:, :, 0], 0.0, 0.5, ALU.is_ge, ALU.subtract)
+        inv_taxi = small("inv_taxi", H)
+        vec.reciprocal(out=inv_taxi[:], in_=taxi_safe[:])
+        signed_a3 = mul("signed_a3", third[:, :, 1], half_sign3[:])
+        terms = [small("terms%d" % n, H, 3) for n in range(NEWTON_STEPS + 1)]
+        vec.tensor_tensor(out=terms[0][:, :, 2], in0=signed_a3[:], in1=inv_taxi[:], op=ALU.mult)
+        norm = fused("norm", half_sign3[:], 2.0, inv_radius[:], ALU.mult, ALU.mult)
+        unit = small("unit", H, 2)
+        vec.tensor_tensor(out=unit[:], in0=third, in1=norm[:].unsqueeze(2).to_broadcast([P, H, 2]), op=ALU.mult)
+        b3 = mul("b3", radius2[:], norm[:])
+
+        def newton(n):
+            angle = terms[n][:, :, 2]
+            pair = small("newton_trig%d" % n, H, 2)
+            act.activation(out=pair[:, :, 0], in_=angle, func=ACT.Sin, scale=-1.0)
+            act.activation(out=pair[:, :, 1], in_=angle, func=ACT.Sin, bias=math.pi / 2)
+            vec.tensor_tensor(out=terms[n][:, :, 0:2], in0=pair[:], in1=unit[:], op=ALU.mult)
+            vec.tensor_reduce(out=terms[n + 1][:, :, 2], in_=terms[n][:], op=ALU.add, axis=AXIS_X)
+
+        for n in range(NEWTON_STEPS):
+            newton(n)
+        angle3 = terms[NEWTON_STEPS][:, :, 2]
+        turn_bias = scaled("turn_bias", angle3, 1.0 / (6.0 * math.pi))
+        lead = scaled("lead", b3[:], -4.0)
+        phase = scaled("phase", angle3, 1.0 / 3.0)
+        inv_lead = small("inv_lead", H)
+        vec.reciprocal(out=inv_lead[:], in_=lead[:])
+
+        trig = small("trig", 2, H, 3)
+        for m in range(2):
+            share = (m + 1) / 3.0
+            act.activation(out=trig[:, m, :, 0], in_=angle3, func=ACT.Sin, scale=-share)
+            act.activation(out=trig[:, m, :, 1], in_=angle3, func=ACT.Sin, scale=share, bias=math.pi / 2)
+            act.activation(out=trig[:, m, :, 2], in_=angle3, func=ACT.Sin, scale=share)
+
+        head_jobs = [k_job(0, 0), q_job(0), k_job(0, 1), k_job(0, 2), k_job(0, 3), q_job(1)]
+        head_tags = ["sum", "sum", "out", "turn", "sum", "sum"]
+        staged = []
+        for n, job in enumerate(head_jobs):
+            staged.append(turned_copy(turn(job, head_tags[n]), vec if n % 2 else act))
+            if n >= 1:
+                quantize(head_jobs[n - 1][1], head_jobs[n - 1][2], staged[n - 1][:])
+
+        products = small("products", 2, 2, H, 2)
+        for j in range(2):
+            vec.tensor_tensor(out=products[:, j, :, :, :], in0=ba[:, 0:2, :, :], in1=trig[:, :, :, j:j + 2], op=ALU.mult)
+        quantize(head_jobs[-1][1], head_jobs[-1][2], staged[-1][:])
+        rotated = small("rotated", 2, 2, H)
+        vec.tensor_reduce(out=rotated[:].rearrange("p j m h -> p (j m h)"),
+                          in_=products[:].rearrange("p j m h x -> p (j m h) x"), op=ALU.add, axis=AXIS_X)
+        a1, a2 = rotated[:, 0, 0, :], rotated[:, 0, 1, :]
+        b1, b2_plain = rotated[:, 1, 0, :], rotated[:, 1, 1, :]
+        half_sign2 = affine("half_sign2", b2_plain, 0.0, 0.5, ALU.is_ge, ALU.subtract)
+        rho2 = fused("rho2", a2, -2.0, inv_lead[:], ALU.mult, ALU.mult)
+        linear0 = fused("linear0", b3[:], 3.0, b1, ALU.mult, ALU.add)
+        eps = fused("eps", half_sign2[:], 4.0, half_sign3[:], ALU.mult, ALU.mult)
+        b2 = fused("b2", half_sign2[:], 2.0 * FLOOR, b2_plain, ALU.mult, ALU.add)
+        gain_lead = small("gain_lead", H * PASSES, PACK)
+        for h in range(H):
+            rows = slice(h * PASSES, (h + 1) * PASSES)
+            vec.tensor_scalar(out=gain_lead[:, rows, :], in0=gain_sb[:, rows, :], scalar1=lead[:, h:h + 1], scalar2=None, op0=ALU.mult)
+        psi = affine("psi", eps[:], -math.pi / 4, math.pi / 4, ALU.mult, ALU.add)
+        eps_b2 = mul("eps_b2", eps[:], b2[:])
+        half_bias = fused("half_bias", phase[:], 0.5, psi[:], ALU.mult, ALU.add)
+        eps_a1 = mul("eps_a1", eps[:], a1)
+        inv_b2 = small("inv_b2", H)
+        vec.reciprocal(out=inv_b2[:], in_=b2[:])
+        sigma = fused("sigma", eps_b2[:], -4.0, inv_lead[:], ALU.mult, ALU.mult)
+        linear1 = fused("linear1", eps_b2[:], 2.0, linear0[:], ALU.mult, ALU.add)
+        const0 = small("const0", H)
+        vec.tensor_tensor(out=const0[:], in0=eps_a1[:], in1=a2, op=ALU.add)
+        root_sigma = small("root_sigma", H)
+        pool_engine.tensor_tensor(out=root_sigma[:], in0=sigma[:], in1=exponent[:, 1, :], op=ALU.pow)
+        rho = fused("rho", a1, 0.5, inv_b2[:], ALU.mult, ALU.mult)
+        rho1 = mul("rho1", linear1[:], inv_lead[:])
+        kappa = mul("kappa", const0[:], inv_lead[:])
+
+        def wide(name, dtype=F32, bufs=2):
+            return work.tile([P, TK], dtype, name=name, bufs=bufs, align_bytes=64)
+
+        st = [dict() for i in range(TILES)]
+
+        def head_col(tile_, i):
+            h = i // Q_TILES
+            return tile_[:, h:h + 1]
+
+        def scores(i):
+            h = i // Q_TILES
+            cols = slice((i % 2) * P, (i % 2 + 1) * P)
+            st[i]["score"] = []
+            for c in range(PASSES):
+                bank = psum.tile([P, K_PASS], F32, name="score_bank", tag="score", bufs=BANKS["score"])
+                pe.matmul_mx(out=bank[:], lhsT=q_codes[i // 2][:, cols].bitcast(FP8X4), lhsT_scale=q_scales[i // 2][:, cols],
+                             rhs=k_codes[h][c][:].bitcast(FP8X4), rhs_scale=k_scales[h][c][:], start=True, stop=True)
+                st[i]["score"].append(bank)
+
+        def turns(i):
+            u = wide("turns", bufs=3)
+            for c in range(PASSES):
+                act.activation(out=u[:, c * K_PASS:(c + 1) * K_PASS], in_=st[i]["score"][c][:], func=ACT.Identity,
+                               scale=1.0 / (2.0 * math.pi * math.sqrt(E)), bias=head_col(turn_bias, i))
+            st[i]["u"] = u
+
+        def whole(i, home):
+            n = home[:].bitcast(I32)
+            if WHOLE_ON_POOL:
+                pool_engine.tensor_scalar(out=n, in0=st[i]["u"][:], scalar1=1.0, scalar2=0.0, op0=ALU.mult, op1=ALU.add)
+            else:
+                vec.tensor_copy(out=n, in_=st[i]["u"][:])
+            st[i]["n"] = n
+
+        def rest(i):
+            r = wide("rest", bufs=3)
+            for c in range(PASSES):
+                cols = slice(c * K_PASS, (c + 1) * K_PASS)
+                vec.scalar_tensor_tensor(out=r[:, cols], in0=st[i]["n"][:, cols], scalar=-2.0 * math.pi * math.sqrt(E),
+                                         in1=st[i]["score"][c][:], op0=ALU.mult, op1=ALU.add)
+            st[i]["r"] = r
+
+        def sine(i):
+            x = wide("x", bufs=3)
+            act.activation(out=x[:], in_=st[i]["r"][:], func=ACT.Sin, scale=1.0 / math.sqrt(E), bias=head_col(phase, i))
+            st[i]["x"] = x
+
+        def half_sine(i):
+            half = wide("half")
+            act.activation(out=half[:], in_=st[i]["r"][:], func=ACT.Sin, scale=0.5 / math.sqrt(E), bias=head_col(half_bias, i))
+            w = wide("w", bufs=3)
+            act.activation(out=w[:], in_=half[:], func=ACT.Square, scale=head_col(root_sigma, i))
+            st[i]["w"] = w
+
+        def shifted_product(i, name, a, shift, b, cols):
+            if name not in st[i]:
+                st[i][name] = wide(name)
+            vec.scalar_tensor_tensor(out=st[i][name][:, cols], in0=st[i][a][:, cols], scalar=head_col(shift, i),
+                                     in1=st[i][b][:, cols], op0=ALU.add, op1=ALU.mult)
+
+        def products_of(i, cols):
+            shifted_product(i, "square", "x", rho2, "x", cols)
+            shifted_product(i, "mixed", "x", rho, "w", cols)
+            shifted_product(i, "cubic", "square", rho1, "x", cols)
+
+        def sum_turned(i, c, tag):
+            bank = psum.tile([P, PACK, P], F32, name="sum_bank", tag=tag, bufs=BANKS[tag])
+            for t in range(PACK):
+                cols = slice((c * PACK + t) * P, (c * PACK + t + 1) * P)
+                pe.matmul(out=bank[:, t, :], lhsT=st[i]["mixed"][:, cols], rhs=ident[:], is_transpose=True, start=True, stop=False)
+                pe.matmul(out=bank[:, t, :], lhsT=st[i]["cubic"][:, cols], rhs=ident[:], is_transpose=True, start=False, stop=True)
+            st[i].setdefault("sum", []).append(bank)
+
+        def gained(i):
+            h = i // Q_TILES
+            ag = wide("ag", BF16)
+            for c in range(PASSES):
+                row = h * PASSES + c
+                vec.scalar_tensor_tensor(
+                    out=ag[:, c * K_PASS:(c + 1) * K_PASS].rearrange("p (r t) -> p r t", t=PACK),
+                    in0=st[i]["sum"][c][:].rearrange("p t r -> p r t"), scalar=head_col(kappa, i),
+                    in1=gain_lead[:, row:row + 1, :].to_broadcast([P, P, PACK]), op0=ALU.add, op1=ALU.mult)
+            st[i]["ag"] = ag
+
+        def quantize_ag(i):
+            codes = work.tile([P, PASSES * P], U32, name="ag_codes", align_bytes=64)
+            scales = work.tile([P, PASSES * P], U8, name="ag_scales", align_bytes=64)
+            quantize(codes[:], scales[:], st[i]["ag"][:])
+            st[i]["codes"], st[i]["scales"] = codes, scales
+
+        def mix_values(i):
+            h = i // Q_TILES
+            bank = psum.tile([P, DV], F32, name="out_bank", tag="out", bufs=BANKS["out"])
+            for c in range(PASSES):
+                cols = slice(c * P, (c + 1) * P)
+                pe.matmul_mx(out=bank[:], lhsT=st[i]["codes"][:, cols].bitcast(FP8X4), lhsT_scale=st[i]["scales"][:, cols],
+                             rhs=v_codes[h][c][:].bitcast(FP8X4), rhs_scale=v_scales[h][c][:], start=(c == 0), stop=(c == PASSES - 1))
+            st[i]["out"] = bank
+
+        def store(i):
+            h, row = divmod(i, Q_TILES)
+            result = work.tile([P, DV], F32, name="result", bufs=3)
+            act.activation(out=result[:], in_=st[i]["out"][:], func=ACT.Copy, scale=1.0 / math.sqrt(TK))
+            dma.dma_start(out=out[h, row * P:(row + 1) * P, :], in_=result[:])
+
+        loop_jobs = [q_job(2), q_job(3)] + [k_job(1, j) for j in range(2 * PASSES)] + [q_job(j) for j in range(4, TILES // 2)]
+        job_bank = {}
+        job_staged = {}
+        v_state = {}
+        V1_START = Q_TILES
+
+        def live(i):
+            return 0 <= i < TILES
+
+        last = TILES - 1
+        for s in range(TILES + 5):
+            if live(s):
+                scores(s)
+            if live(s - 5):
+                mix_values(s - 5)
+            if s - 1 in job_bank:
+                job_staged[s - 1] = turned_copy(job_bank[s - 1], act)
+            if live(s - 2):
+                sine(s - 2)
+            if live(s):
+                turns(s)
+            if live(s - 2):
+                half_sine(s - 2)
+            if live(s - 5):
+                store(s - 5)
+            if 0 <= s - V1_START < 2 * PASSES:
+                c, second = divmod(s - V1_START, 2)
+                v_state[c] = interleave_v(v_state[c], act) if second else widen_v(1, c, act)
+            if s < len(loop_jobs):
+                job_bank[s] = turn(loop_jobs[s], "turn")
+            if s in (1, 2):
+                rest(s - 1)
+            if s == 0:
+                v_state[0] = interleave_v(widen_v(0, 0, vec), vec)
+            if s == 1:
+                planes1 = widen_v(0, 1, vec)
+                quantize(v_codes[0][0][:], v_scales[0][0][:], v_state[0][:])
+            if s == 2:
+                v_state[1] = interleave_v(planes1, vec)
+            if s - 3 == last:
+                for c in range(PASSES):
+                    products_of(last, slice(c * K_PASS, (c + 1) * K_PASS))
+                    sum_turned(last, c, "score")
+            elif live(s - 3):
+                products_of(s - 3, slice(0, TK))
+            if live(s):
+                if live(s - 3):
+                    home = st[s - 3]["square"]
+                else:
+                    home = wide("square")
+                whole(s, home)
+            if live(s - 4):
+                gained(s - 4)
+            if live(s - 3) and s - 3 != last:
+                for c in range(PASSES):
+                    sum_turned(s - 3, c, "sum")
+            if live(s - 1) and s > 2:
+                rest(s - 1)
+            if s == 3:
+                quantize(v_codes[0][1][:], v_scales[0][1][:], v_state[1][:])
+            if s - 1 in job_staged:
+                quantize(loop_jobs[s - 1][1], loop_jobs[s - 1][2], job_staged[s - 1][:])
+            if s - V1_START in (2, 4):
+                c = (s - V1_START) // 2 - 1
+                quantize(v_codes[1][c][:], v_scales[1][c][:], v_state[c][:])
+            if live(s - 4):
+                quantize_ag(s - 4)

@@ -25,7 +25,7 @@ PASSES = TK // K_PASS
 Q_TILES = TQ // P
 TILES = H * Q_TILES
 NEWTON_STEPS = 2
-WHOLE_ON_POOL = True
+EARLY = 1
 FLOOR = 2.0 ** -60
 BANKS = {"score": 4, "sum": 2, "out": 1, "turn": 1}
 
@@ -68,10 +68,11 @@ def tile_fourierkolmogorovarnoldattention_kernel(tc, q, k, v_bytes, v_scale, ca,
         act.dma_start(out=cb_sb[:], in_=cb.rearrange("h m -> (h m)").partition_broadcast(P))
         load_k(0, 0)
         load_q(0)
-        for j in range(1, 2 * PASSES):
-            load_k(0, j)
+        load_k(0, 1)
         dma.dma_start(out=v_scale_sb[:], in_=v_scale.rearrange("o (c p t) x -> p (o c) (t x)", p=P, t=PACK))
         load_v(0, 0)
+        load_k(0, 2)
+        load_k(0, 3)
         load_q(1)
         load_v(0, 1)
         dma.dma_start(out=gain_sb[:], in_=g.rearrange("h (c p t) -> p (h c) t", p=P, t=PACK))
@@ -129,25 +130,26 @@ def tile_fourierkolmogorovarnoldattention_kernel(tc, q, k, v_bytes, v_scale, ca,
         def quantize(codes, scales, values):
             vec.quantize_mx(out=codes.bitcast(FP8X4), scales=scales, in_=values)
 
-        def widen_v(h, c, engine):
-            planes = work.tile([P, PACK, DV], BF16, name="v_planes", align_bytes=64)
-            for t in range(PACK):
-                src = v_raw[h][c][:, t * DV:(t + 1) * DV].bitcast(FP8)
-                if engine is act:
-                    act.activation(out=planes[:, t, :], in_=src, func=ACT.Copy, scale=v_scale_sb[:, c, t:t + 1])
-                else:
-                    vec.tensor_scalar(out=planes[:, t, :], in0=src, scalar1=v_scale_sb[:, c, t:t + 1], scalar2=None, op0=ALU.mult)
-            return planes
+        def v_planes_tile():
+            return work.tile([P, PACK, DV], BF16, name="v_planes", align_bytes=64)
 
-        def interleave_v(planes, engine):
-            woven = work.tile([P, DV * PACK], BF16, name="v_woven", align_bytes=64)
-            dst = woven[:].rearrange("p (n t) -> p n t", t=PACK)
-            src = planes[:].rearrange("p t n -> p n t")
+        def v_woven_tile():
+            return work.tile([P, DV * PACK], BF16, name="v_woven", align_bytes=64)
+
+        def widen_v(h, c, t, planes, engine):
+            src = v_raw[h][c][:, t * DV:(t + 1) * DV].bitcast(FP8)
+            if engine is act:
+                act.activation(out=planes[:, t, :], in_=src, func=ACT.Copy, scale=v_scale_sb[:, c, t:t + 1])
+            else:
+                vec.tensor_scalar(out=planes[:, t, :], in0=src, scalar1=v_scale_sb[:, c, t:t + 1], scalar2=None, op0=ALU.mult)
+
+        def interleave_v(planes, woven, cols, engine):
+            dst = woven[:].rearrange("p (n t) -> p n t", t=PACK)[:, cols, :].rearrange("p (c i) t -> p c t i", i=4)
+            src = planes[:, :, cols].rearrange("p t (c i) -> p c t i", i=4)
             if engine is act:
                 act.copy(out=dst, in_=src)
             else:
                 vec.tensor_copy(out=dst, in_=src)
-            return woven
 
         def small(name, *shape):
             return kept(name, [P] + list(shape), F32)
@@ -195,22 +197,39 @@ def tile_fourierkolmogorovarnoldattention_kernel(tc, q, k, v_bytes, v_scale, ca,
         vec.tensor_tensor(out=unit[:], in0=third, in1=norm[:].unsqueeze(2).to_broadcast([P, H, 2]), op=ALU.mult)
         b3 = mul("b3", radius2[:], norm[:])
 
-        def newton(n):
+        def newton(n, filler):
             angle = terms[n][:, :, 2]
             pair = small("newton_trig%d" % n, H, 2)
             act.activation(out=pair[:, :, 0], in_=angle, func=ACT.Sin, scale=-1.0)
             act.activation(out=pair[:, :, 1], in_=angle, func=ACT.Sin, bias=math.pi / 2)
             vec.tensor_tensor(out=terms[n][:, :, 0:2], in0=pair[:], in1=unit[:], op=ALU.mult)
+            filler()
             vec.tensor_reduce(out=terms[n + 1][:, :, 2], in_=terms[n][:], op=ALU.add, axis=AXIS_X)
 
-        for n in range(NEWTON_STEPS):
-            newton(n)
-        angle3 = terms[NEWTON_STEPS][:, :, 2]
-        turn_bias = scaled("turn_bias", angle3, 1.0 / (6.0 * math.pi))
+        head_jobs = [k_job(0, 0), q_job(0), k_job(0, 1), k_job(0, 2), k_job(0, 3)]
+        head_tags = ["sum", "sum", "out", "turn", "sum"]
+
+        def head_copy(n, engine):
+            return turned_copy(turn(head_jobs[n], head_tags[n]), engine)
+
+        def head_quantize(n, grouped):
+            quantize(head_jobs[n][1], head_jobs[n][2], grouped[:])
+
+        planes0 = [v_planes_tile(), v_planes_tile()]
+        woven0 = [v_woven_tile(), v_woven_tile()]
         lead = scaled("lead", b3[:], -4.0)
-        phase = scaled("phase", angle3, 1.0 / 3.0)
         inv_lead = small("inv_lead", H)
-        vec.reciprocal(out=inv_lead[:], in_=lead[:])
+        newton(0, lambda: vec.reciprocal(out=inv_lead[:], in_=lead[:]))
+        staged0 = head_copy(0, act)
+        widen_v(0, 0, 0, planes0[0], vec)
+        newton(1, lambda: head_quantize(0, staged0))
+        staged1 = head_copy(1, act)
+        angle3 = terms[NEWTON_STEPS][:, :, 2]
+        widen_v(0, 0, 1, planes0[0], vec)
+        turn_bias = scaled("turn_bias", angle3, 1.0 / (6.0 * math.pi))
+        phase = scaled("phase", angle3, 1.0 / 3.0)
+        staged2 = head_copy(2, vec)
+        head_quantize(1, staged1)
 
         trig = small("trig", 2, H, 3)
         for m in range(2):
@@ -218,46 +237,44 @@ def tile_fourierkolmogorovarnoldattention_kernel(tc, q, k, v_bytes, v_scale, ca,
             act.activation(out=trig[:, m, :, 0], in_=angle3, func=ACT.Sin, scale=-share)
             act.activation(out=trig[:, m, :, 1], in_=angle3, func=ACT.Sin, scale=share, bias=math.pi / 2)
             act.activation(out=trig[:, m, :, 2], in_=angle3, func=ACT.Sin, scale=share)
-
-        head_jobs = [k_job(0, 0), q_job(0), k_job(0, 1), k_job(0, 2), k_job(0, 3), q_job(1)]
-        head_tags = ["sum", "sum", "out", "turn", "sum", "sum"]
-        staged = []
-        for n, job in enumerate(head_jobs):
-            staged.append(turned_copy(turn(job, head_tags[n]), vec if n % 2 else act))
-            if n >= 1:
-                quantize(head_jobs[n - 1][1], head_jobs[n - 1][2], staged[n - 1][:])
+        staged3 = head_copy(3, act)
+        staged4 = head_copy(4, act)
+        head_quantize(2, staged2)
 
         products = small("products", 2, 2, H, 2)
         for j in range(2):
             vec.tensor_tensor(out=products[:, j, :, :, :], in0=ba[:, 0:2, :, :], in1=trig[:, :, :, j:j + 2], op=ALU.mult)
-        quantize(head_jobs[-1][1], head_jobs[-1][2], staged[-1][:])
+        head_quantize(3, staged3)
         rotated = small("rotated", 2, 2, H)
         vec.tensor_reduce(out=rotated[:].rearrange("p j m h -> p (j m h)"),
                           in_=products[:].rearrange("p j m h x -> p (j m h) x"), op=ALU.add, axis=AXIS_X)
         a1, a2 = rotated[:, 0, 0, :], rotated[:, 0, 1, :]
         b1, b2_plain = rotated[:, 1, 0, :], rotated[:, 1, 1, :]
+        widen_v(0, 0, 2, planes0[0], vec)
         half_sign2 = affine("half_sign2", b2_plain, 0.0, 0.5, ALU.is_ge, ALU.subtract)
         rho2 = fused("rho2", a2, -2.0, inv_lead[:], ALU.mult, ALU.mult)
         linear0 = fused("linear0", b3[:], 3.0, b1, ALU.mult, ALU.add)
+        head_quantize(4, staged4)
         eps = fused("eps", half_sign2[:], 4.0, half_sign3[:], ALU.mult, ALU.mult)
         b2 = fused("b2", half_sign2[:], 2.0 * FLOOR, b2_plain, ALU.mult, ALU.add)
+        widen_v(0, 0, 3, planes0[0], vec)
+        eps_b2 = mul("eps_b2", eps[:], b2[:])
+        psi = affine("psi", eps[:], -math.pi / 4, math.pi / 4, ALU.mult, ALU.add)
+        eps_a1 = mul("eps_a1", eps[:], a1)
+        inv_b2 = small("inv_b2", H)
+        vec.reciprocal(out=inv_b2[:], in_=b2[:])
         gain_lead = small("gain_lead", H * PASSES, PACK)
         for h in range(H):
             rows = slice(h * PASSES, (h + 1) * PASSES)
             vec.tensor_scalar(out=gain_lead[:, rows, :], in0=gain_sb[:, rows, :], scalar1=lead[:, h:h + 1], scalar2=None, op0=ALU.mult)
-        psi = affine("psi", eps[:], -math.pi / 4, math.pi / 4, ALU.mult, ALU.add)
-        eps_b2 = mul("eps_b2", eps[:], b2[:])
-        half_bias = fused("half_bias", phase[:], 0.5, psi[:], ALU.mult, ALU.add)
-        eps_a1 = mul("eps_a1", eps[:], a1)
-        inv_b2 = small("inv_b2", H)
-        vec.reciprocal(out=inv_b2[:], in_=b2[:])
         sigma = fused("sigma", eps_b2[:], -4.0, inv_lead[:], ALU.mult, ALU.mult)
+        half_bias = fused("half_bias", phase[:], 0.5, psi[:], ALU.mult, ALU.add)
         linear1 = fused("linear1", eps_b2[:], 2.0, linear0[:], ALU.mult, ALU.add)
         const0 = small("const0", H)
         vec.tensor_tensor(out=const0[:], in0=eps_a1[:], in1=a2, op=ALU.add)
+        rho = fused("rho", a1, 0.5, inv_b2[:], ALU.mult, ALU.mult)
         root_sigma = small("root_sigma", H)
         pool_engine.tensor_tensor(out=root_sigma[:], in0=sigma[:], in1=exponent[:, 1, :], op=ALU.pow)
-        rho = fused("rho", a1, 0.5, inv_b2[:], ALU.mult, ALU.mult)
         rho1 = mul("rho1", linear1[:], inv_lead[:])
         kappa = mul("kappa", const0[:], inv_lead[:])
 
@@ -280,19 +297,18 @@ def tile_fourierkolmogorovarnoldattention_kernel(tc, q, k, v_bytes, v_scale, ca,
                              rhs=k_codes[h][c][:].bitcast(FP8X4), rhs_scale=k_scales[h][c][:], start=True, stop=True)
                 st[i]["score"].append(bank)
 
-        def turns(i):
-            u = wide("turns", bufs=3)
-            for c in range(PASSES):
-                act.activation(out=u[:, c * K_PASS:(c + 1) * K_PASS], in_=st[i]["score"][c][:], func=ACT.Identity,
-                               scale=1.0 / (2.0 * math.pi * math.sqrt(E)), bias=head_col(turn_bias, i))
-            st[i]["u"] = u
+        def turns(i, c):
+            if c == 0:
+                st[i]["u"] = wide("turns", bufs=3)
+            act.activation(out=st[i]["u"][:, c * K_PASS:(c + 1) * K_PASS], in_=st[i]["score"][c][:], func=ACT.Identity,
+                           scale=1.0 / (2.0 * math.pi * math.sqrt(E)), bias=head_col(turn_bias, i))
 
-        def whole(i, home):
+        def whole(i, home, engine):
             n = home[:].bitcast(I32)
-            if WHOLE_ON_POOL:
-                pool_engine.tensor_scalar(out=n, in0=st[i]["u"][:], scalar1=1.0, scalar2=0.0, op0=ALU.mult, op1=ALU.add)
-            else:
+            if engine is vec:
                 vec.tensor_copy(out=n, in_=st[i]["u"][:])
+            else:
+                pool_engine.tensor_scalar(out=n, in0=st[i]["u"][:], scalar1=1.0, scalar2=0.0, op0=ALU.mult, op1=ALU.add)
             st[i]["n"] = n
 
         def rest(i):
@@ -311,8 +327,11 @@ def tile_fourierkolmogorovarnoldattention_kernel(tc, q, k, v_bytes, v_scale, ca,
         def half_sine(i):
             half = wide("half")
             act.activation(out=half[:], in_=st[i]["r"][:], func=ACT.Sin, scale=0.5 / math.sqrt(E), bias=head_col(half_bias, i))
+            st[i]["half"] = half
+
+        def squared(i):
             w = wide("w", bufs=3)
-            act.activation(out=w[:], in_=half[:], func=ACT.Square, scale=head_col(root_sigma, i))
+            act.activation(out=w[:], in_=st[i]["half"][:], func=ACT.Square, scale=head_col(root_sigma, i))
             st[i]["w"] = w
 
         def shifted_product(i, name, a, shift, b, cols):
@@ -334,26 +353,30 @@ def tile_fourierkolmogorovarnoldattention_kernel(tc, q, k, v_bytes, v_scale, ca,
                 pe.matmul(out=bank[:, t, :], lhsT=st[i]["cubic"][:, cols], rhs=ident[:], is_transpose=True, start=False, stop=True)
             st[i].setdefault("sum", []).append(bank)
 
-        def gained(i):
+        def gained(i, passes=range(PASSES)):
             h = i // Q_TILES
-            ag = wide("ag", BF16)
-            for c in range(PASSES):
+            if "ag" not in st[i]:
+                st[i]["ag"] = wide("ag", BF16)
+            ag = st[i]["ag"]
+            for c in passes:
                 row = h * PASSES + c
                 vec.scalar_tensor_tensor(
                     out=ag[:, c * K_PASS:(c + 1) * K_PASS].rearrange("p (r t) -> p r t", t=PACK),
                     in0=st[i]["sum"][c][:].rearrange("p t r -> p r t"), scalar=head_col(kappa, i),
                     in1=gain_lead[:, row:row + 1, :].to_broadcast([P, P, PACK]), op0=ALU.add, op1=ALU.mult)
-            st[i]["ag"] = ag
 
-        def quantize_ag(i):
-            codes = work.tile([P, PASSES * P], U32, name="ag_codes", align_bytes=64)
-            scales = work.tile([P, PASSES * P], U8, name="ag_scales", align_bytes=64)
-            quantize(codes[:], scales[:], st[i]["ag"][:])
+        def quantize_ag(i, parts=1):
+            codes = work.tile([P, PASSES * P], U32, name="ag_codes", align_bytes=64, bufs=6)
+            scales = work.tile([P, PASSES * P], U8, name="ag_scales", align_bytes=64, bufs=6)
+            width = PASSES * P // parts
+            for j in range(parts):
+                cols = slice(j * width, (j + 1) * width)
+                quantize(codes[:, cols], scales[:, cols], st[i]["ag"][:, j * width * PACK:(j + 1) * width * PACK])
             st[i]["codes"], st[i]["scales"] = codes, scales
 
-        def mix_values(i):
+        def mix_values(i, tag="out"):
             h = i // Q_TILES
-            bank = psum.tile([P, DV], F32, name="out_bank", tag="out", bufs=BANKS["out"])
+            bank = psum.tile([P, DV], F32, name="out_bank", tag=tag, bufs=BANKS[tag])
             for c in range(PASSES):
                 cols = slice(c * P, (c + 1) * P)
                 pe.matmul_mx(out=bank[:], lhsT=st[i]["codes"][:, cols].bitcast(FP8X4), lhsT_scale=st[i]["scales"][:, cols],
@@ -366,70 +389,138 @@ def tile_fourierkolmogorovarnoldattention_kernel(tc, q, k, v_bytes, v_scale, ca,
             act.activation(out=result[:], in_=st[i]["out"][:], func=ACT.Copy, scale=1.0 / math.sqrt(TK))
             dma.dma_start(out=out[h, row * P:(row + 1) * P, :], in_=result[:])
 
-        loop_jobs = [q_job(2), q_job(3)] + [k_job(1, j) for j in range(2 * PASSES)] + [q_job(j) for j in range(4, TILES // 2)]
+        loop_jobs = [q_job(3)] + [k_job(1, j) for j in range(2 * PASSES)] + [q_job(j) for j in range(4, TILES // 2)]
+        JOB_START = 1
         job_bank = {}
         job_staged = {}
-        v_state = {}
-        V1_START = Q_TILES
+        planes1 = []
+        woven1 = []
+        WIDEN_START = 3
+        WEAVE_START = WIDEN_START + PASSES * PACK
+        V1_READY = WEAVE_START + 2 * PASSES + 1
+        mix_step = {i: i + 5 for i in range(Q_TILES)}
+        for i in range(Q_TILES, TILES):
+            mix_step[i] = max(i + 5, V1_READY + (i - Q_TILES) // 2)
 
         def live(i):
             return 0 <= i < TILES
 
         last = TILES - 1
-        for s in range(TILES + 5):
+        scores(0)
+        scores(1)
+        bank_q1 = turn(q_job(1), "sum")
+        bank_q2 = turn(q_job(2), "sum")
+        job_bank[JOB_START] = turn(loop_jobs[0], "turn")
+        for i in range(2):
+            for c in range(PASSES):
+                turns(i, c)
+        staged_q1 = turned_copy(bank_q1, act)
+        whole(0, wide("square"), vec)
+        interleave_v(planes0[0], woven0[0], slice(0, DV // 2), vec)
+        rest(0)
+        whole(1, wide("square"), vec)
+        quantize(q_job(1)[1], q_job(1)[2], staged_q1[:])
+        rest(1)
+        for s in range(2, TILES + 3):
+            mixes = [i for i in range(last - 2) if mix_step[i] == s]
             if live(s):
                 scores(s)
-            if live(s - 5):
-                mix_values(s - 5)
+            if mixes:
+                mix_values(mixes[0])
+            if live(s - 4) and s - 4 != last:
+                for c in range(EARLY, PASSES):
+                    sum_turned(s - 4, c, "sum")
             if s - 1 in job_bank:
                 job_staged[s - 1] = turned_copy(job_bank[s - 1], act)
+            if s - JOB_START < len(loop_jobs):
+                job_bank[s] = turn(loop_jobs[s - JOB_START], "turn")
             if live(s - 2):
                 sine(s - 2)
-            if live(s):
-                turns(s)
-            if live(s - 2):
-                half_sine(s - 2)
-            if live(s - 5):
-                store(s - 5)
-            if 0 <= s - V1_START < 2 * PASSES:
-                c, second = divmod(s - V1_START, 2)
-                v_state[c] = interleave_v(v_state[c], act) if second else widen_v(1, c, act)
-            if s < len(loop_jobs):
-                job_bank[s] = turn(loop_jobs[s], "turn")
-            if s in (1, 2):
-                rest(s - 1)
-            if s == 0:
-                v_state[0] = interleave_v(widen_v(0, 0, vec), vec)
-            if s == 1:
-                planes1 = widen_v(0, 1, vec)
-                quantize(v_codes[0][0][:], v_scales[0][0][:], v_state[0][:])
             if s == 2:
-                v_state[1] = interleave_v(planes1, vec)
+                half_sine(0)
+            if live(s):
+                turns(s, 0)
+            if s == 2:
+                squared(0)
+            elif live(s - 2):
+                half_sine(s - 2)
+            if live(s):
+                turns(s, 1)
+            elif mixes:
+                store(mixes[0])
+                mixes = mixes[1:]
+                if mixes:
+                    mix_values(mixes[0])
+            if live(s - 2) and s > 2:
+                squared(s - 2)
+            if mixes:
+                store(mixes[0])
+            if 0 <= s - WIDEN_START < PASSES * PACK:
+                c, t = divmod(s - WIDEN_START, PACK)
+                if t == 0:
+                    planes1.append(v_planes_tile())
+                widen_v(1, c, t, planes1[c], act)
+            if 0 <= s - WEAVE_START < 2 * PASSES:
+                c, part = divmod(s - WEAVE_START, 2)
+                if part == 0:
+                    woven1.append(v_woven_tile())
+                interleave_v(planes1[c], woven1[c], slice(part * DV // 2, (part + 1) * DV // 2), act)
+            if s == 2:
+                interleave_v(planes0[0], woven0[0], slice(DV // 2, DV), vec)
+                staged_q2 = turned_copy(bank_q2, vec)
+                for t in range(PACK):
+                    widen_v(0, 1, t, planes0[1], vec)
+                quantize(v_codes[0][0][:], v_scales[0][0][:], woven0[0][:])
+                interleave_v(planes0[1], woven0[1], slice(0, DV), vec)
+                quantize(q_job(2)[1], q_job(2)[2], staged_q2[:])
             if s - 3 == last:
                 for c in range(PASSES):
                     products_of(last, slice(c * K_PASS, (c + 1) * K_PASS))
                     sum_turned(last, c, "score")
+                    if c == 0:
+                        quantize_ag(last - 2)
             elif live(s - 3):
                 products_of(s - 3, slice(0, TK))
-            if live(s):
-                if live(s - 3):
-                    home = st[s - 3]["square"]
-                else:
-                    home = wide("square")
-                whole(s, home)
+            if live(s) and live(s - 3):
+                whole(s, st[s - 3]["square"], pool_engine)
             if live(s - 4):
                 gained(s - 4)
             if live(s - 3) and s - 3 != last:
-                for c in range(PASSES):
+                for c in range(EARLY):
                     sum_turned(s - 3, c, "sum")
             if live(s - 1) and s > 2:
                 rest(s - 1)
             if s == 3:
-                quantize(v_codes[0][1][:], v_scales[0][1][:], v_state[1][:])
-            if s - 1 in job_staged:
-                quantize(loop_jobs[s - 1][1], loop_jobs[s - 1][2], job_staged[s - 1][:])
-            if s - V1_START in (2, 4):
-                c = (s - V1_START) // 2 - 1
-                quantize(v_codes[1][c][:], v_scales[1][c][:], v_state[c][:])
-            if live(s - 4):
+                quantize(v_codes[0][1][:], v_scales[0][1][:], woven0[1][:])
+            if live(s - 4) and live(s - 1):
                 quantize_ag(s - 4)
+            if s - 1 in job_staged:
+                quantize(loop_jobs[s - 1 - JOB_START][1], loop_jobs[s - 1 - JOB_START][2], job_staged[s - 1][:])
+            if s - WEAVE_START in (2, 4):
+                c = (s - WEAVE_START) // 2 - 1
+                quantize(v_codes[1][c][:], v_scales[1][c][:], woven1[c][:])
+            if s < 3:
+                whole(s, wide("square"), vec)
+        mix_values(last - 2, "turn")
+        gained(last, [0])
+        quantize_ag(last - 1)
+        gained(last, [1])
+        store(last - 2)
+        mix_values(last - 1)
+        quantize_ag(last, PASSES)
+        store(last - 1)
+        h, row = divmod(last, Q_TILES)
+        for part in range(2):
+            cols = slice(part * DV // 2, (part + 1) * DV // 2)
+            bank = psum.tile([P, DV // 2], F32, name="last_bank", tag="score", bufs=BANKS["score"])
+            for c in range(PASSES):
+                rows = slice(c * P, (c + 1) * P)
+                pe.matmul_mx(out=bank[:], lhsT=st[last]["codes"][:, rows].bitcast(FP8X4), lhsT_scale=st[last]["scales"][:, rows],
+                             rhs=v_codes[h][c][:, cols].bitcast(FP8X4), rhs_scale=v_scales[h][c][:, cols], start=(c == 0), stop=(c == PASSES - 1))
+            piece = work.tile([P, DV // 2], F32, name="piece")
+            if part == 0:
+                vec.tensor_scalar(out=piece[:], in0=bank[:], scalar1=1.0 / math.sqrt(TK), scalar2=None, op0=ALU.mult)
+                dma.dma_start(out=out[h, row * P:(row + 1) * P, cols], in_=piece[:])
+            else:
+                act.activation(out=piece[:], in_=bank[:], func=ACT.Copy, scale=1.0 / math.sqrt(TK))
+                act.dma_start(out=out[h, row * P:(row + 1) * P, cols], in_=piece[:])

@@ -25,9 +25,8 @@ PASSES = TK // K_PASS
 Q_TILES = TQ // P
 TILES = H * Q_TILES
 NEWTON_STEPS = 2
-EARLY = 1
 FLOOR = 2.0 ** -60
-BANKS = {"score": 4, "sum": 2, "out": 1, "turn": 1}
+BANKS = {"score": 3, "sum": 2, "out": 2, "turn": 1}
 
 
 def tile_fourierkolmogorovarnoldattention_kernel(tc, q, k, v_bytes, v_scale, ca, cb, g, out):
@@ -67,10 +66,10 @@ def tile_fourierkolmogorovarnoldattention_kernel(tc, q, k, v_bytes, v_scale, ca,
         act.dma_start(out=ca_sb[:], in_=ca.rearrange("h m -> (h m)").partition_broadcast(P))
         act.dma_start(out=cb_sb[:], in_=cb.rearrange("h m -> (h m)").partition_broadcast(P))
         load_k(0, 0)
-        load_q(0)
-        load_k(0, 1)
         dma.dma_start(out=v_scale_sb[:], in_=v_scale.rearrange("o (c p t) x -> p (o c) (t x)", p=P, t=PACK))
         load_v(0, 0)
+        load_q(0)
+        load_k(0, 1)
         load_k(0, 2)
         load_k(0, 3)
         load_q(1)
@@ -87,9 +86,8 @@ def tile_fourierkolmogorovarnoldattention_kernel(tc, q, k, v_bytes, v_scale, ca,
 
         ident = kept("ident", [P, P], F32)
         make_identity(nc, ident[:])
-        exponent = kept("exponent", [P, 2, H], F32)
-        pool_engine.memset(exponent[:, 0, :], -0.5)
-        pool_engine.memset(exponent[:, 1, :], 0.5)
+        exponent = kept("exponent", [P, 2 * H], F32)
+        pool_engine.memset(exponent[:], -0.5)
         warm = kept("warm", [P, 2], F32)
         vec.memset(warm[:, 0:1], 0.0)
         act.activation(out=warm[:, 1:2], in_=warm[:, 0:1], func=ACT.Sin)
@@ -106,20 +104,23 @@ def tile_fourierkolmogorovarnoldattention_kernel(tc, q, k, v_bytes, v_scale, ca,
             cols = slice(half * 2 * P, (half + 1) * 2 * P)
             return (k_rows[h][j][:], k_codes[h][c][:, cols], k_scales[h][c][:, cols])
 
-        def q_job(j):
-            return (q_rows[j][:], q_codes[j][:], q_scales[j][:])
+        def q_job(j, first=0, count=2):
+            cols = slice(first * P, (first + count) * P)
+            return (q_rows[j][:, first * E:(first + count) * E], q_codes[j][:, cols], q_scales[j][:, cols])
 
         def turn(job, tag):
             words = job[0].bitcast(F32)
-            bank = psum.tile([P, 2, 2, P], F32, name="turn_bank", tag=tag, bufs=BANKS[tag])
-            for i in range(2):
+            count = words.shape[1] // (E // 2)
+            bank = psum.tile([P, count, 2, P], F32, name="turn_bank", tag=tag, bufs=BANKS[tag])
+            for i in range(count):
                 for u in range(2):
                     pe.transpose(bank[:, i, u, :], words[:, i * (E // 2) + u:(i + 1) * (E // 2):2], ident[:])
             return bank
 
         def turned_copy(bank, engine):
-            grouped = work.tile([P, 2 * P * PACK], BF16, name="grouped", align_bytes=64, bufs=3)
-            dst = grouped[:].bitcast(F32).rearrange("p (i r u) -> p i r u", i=2, u=2)
+            count = bank[:].shape[1]
+            grouped = work.tile([P, count * P * PACK], BF16, name="grouped", align_bytes=64, bufs=5)
+            dst = grouped[:].bitcast(F32).rearrange("p (i r u) -> p i r u", i=count, u=2)
             src = bank[:].rearrange("p i u r -> p i r u")
             if engine is act:
                 act.copy(out=dst, in_=src)
@@ -151,132 +152,160 @@ def tile_fourierkolmogorovarnoldattention_kernel(tc, q, k, v_bytes, v_scale, ca,
             else:
                 vec.tensor_copy(out=dst, in_=src)
 
-        def small(name, *shape):
-            return kept(name, [P] + list(shape), F32)
+        def small(name, *shape, dtype=F32):
+            return kept(name, [P] + list(shape), dtype)
 
-        def mul(name, a, b):
-            o = small(name, H)
-            vec.tensor_tensor(out=o[:], in0=a, in1=b, op=ALU.mult)
+        def binary(name, a, b, op=ALU.mult):
+            o = small(name, *a.shape[1:])
+            vec.tensor_tensor(out=o[:], in0=a, in1=b, op=op)
             return o
 
         def fused(name, a, scalar, b, op0, op1):
-            o = small(name, H)
+            o = small(name, *a.shape[1:])
             vec.scalar_tensor_tensor(out=o[:], in0=a, scalar=scalar, in1=b, op0=op0, op1=op1)
             return o
 
-        def scaled(name, a, factor):
-            o = small(name, H)
-            vec.tensor_scalar(out=o[:], in0=a, scalar1=factor, scalar2=None, op0=ALU.mult)
-            return o
-
-        def affine(name, a, s1, s2, op0, op1):
-            o = small(name, H)
+        def affine(name, a, s1, s2, op0=ALU.mult, op1=ALU.add, dtype=F32):
+            o = small(name, *a.shape[1:], dtype=dtype)
             vec.tensor_scalar(out=o[:], in0=a, scalar1=s1, scalar2=s2, op0=op0, op1=op1)
             return o
 
-        ba = small("ba", HARMONICS, H, 2)
-        vec.tensor_copy(out=ba[:, :, :, 0], in_=cb_sb[:].rearrange("p (h m) -> p m h", h=H))
-        vec.tensor_copy(out=ba[:, :, :, 1], in_=ca_sb[:].rearrange("p (h m) -> p m h", h=H))
-        third = ba[:, 2, :, :]
-        squares = small("squares", H, 2)
-        vec.tensor_tensor(out=squares[:], in0=third, in1=third, op=ALU.mult)
-        taxi = small("taxi", H)
-        vec.tensor_reduce(out=taxi[:], in_=third, op=ALU.add, axis=AXIS_X, apply_absolute_value=True)
-        radius2 = fused("radius2", squares[:, :, 0], FLOOR * FLOOR, squares[:, :, 1], ALU.add, ALU.add)
-        inv_radius = small("inv_radius", H)
-        pool_engine.tensor_tensor(out=inv_radius[:], in0=radius2[:], in1=exponent[:, 0, :], op=ALU.pow)
-        taxi_safe = affine("taxi_safe", taxi[:], FLOOR, 1.0 / math.pi, ALU.add, ALU.mult)
-        half_sign3 = affine("half_sign3", third[:, :, 0], 0.0, 0.5, ALU.is_ge, ALU.subtract)
-        inv_taxi = small("inv_taxi", H)
-        vec.reciprocal(out=inv_taxi[:], in_=taxi_safe[:])
-        signed_a3 = mul("signed_a3", third[:, :, 1], half_sign3[:])
-        terms = [small("terms%d" % n, H, 3) for n in range(NEWTON_STEPS + 1)]
-        vec.tensor_tensor(out=terms[0][:, :, 2], in0=signed_a3[:], in1=inv_taxi[:], op=ALU.mult)
-        norm = fused("norm", half_sign3[:], 2.0, inv_radius[:], ALU.mult, ALU.mult)
-        unit = small("unit", H, 2)
-        vec.tensor_tensor(out=unit[:], in0=third, in1=norm[:].unsqueeze(2).to_broadcast([P, H, 2]), op=ALU.mult)
-        b3 = mul("b3", radius2[:], norm[:])
+        def inverse(name, a):
+            o = small(name, *a.shape[1:])
+            vec.reciprocal(out=o[:], in_=a)
+            return o
 
-        def newton(n, filler):
-            angle = terms[n][:, :, 2]
-            pair = small("newton_trig%d" % n, H, 2)
-            act.activation(out=pair[:, :, 0], in_=angle, func=ACT.Sin, scale=-1.0)
-            act.activation(out=pair[:, :, 1], in_=angle, func=ACT.Sin, bias=math.pi / 2)
+        second, third = slice(0, H), slice(H, 2 * H)
+        ba = small("ba", HARMONICS * H, 2)
+        vec.tensor_copy(out=ba[:, :, 0].rearrange("p (m h) -> p m h", h=H), in_=cb_sb[:].rearrange("p (h m) -> p m h", h=H))
+        vec.tensor_copy(out=ba[:, :, 1].rearrange("p (m h) -> p m h", h=H), in_=ca_sb[:].rearrange("p (h m) -> p m h", h=H))
+        upper = ba[:, H:, :]
+        squares = binary("squares", upper, upper)
+        taxi = small("taxi", 2 * H)
+        vec.tensor_reduce(out=taxi[:], in_=upper, op=ALU.add, axis=AXIS_X, apply_absolute_value=True)
+        half_sign = affine("half_sign", upper[:, :, 0], 0.0, 0.5, ALU.is_ge, ALU.subtract)
+        radius2 = fused("radius2", squares[:, :, 0], FLOOR * FLOOR, squares[:, :, 1], ALU.add, ALU.add)
+        inv_radius = small("inv_radius", 2 * H)
+        pool_engine.tensor_tensor(out=inv_radius[:], in0=radius2[:], in1=exponent[:], op=ALU.pow)
+        taxi_safe = affine("taxi_safe", taxi[:], FLOOR, 1.0 / math.pi, ALU.add, ALU.mult)
+        signed_a = binary("signed_a", upper[:, :, 1], half_sign[:])
+        inv_taxi = inverse("inv_taxi", taxi_safe[:])
+        sign23 = fused("sign23", half_sign[:, second], 4.0, half_sign[:, third], ALU.mult, ALU.mult)
+        terms = [small("terms%d" % n, 2 * H, 3) for n in range(NEWTON_STEPS + 1)]
+        vec.tensor_tensor(out=terms[0][:, :, 2], in0=signed_a[:], in1=inv_taxi[:], op=ALU.mult)
+        planes0 = [v_planes_tile()]
+        woven0 = [v_woven_tile()]
+        norm = fused("norm", half_sign[:], 2.0, inv_radius[:], ALU.mult, ALU.mult)
+        radius = binary("radius", radius2[:], inv_radius[:])
+        widen_v(0, 0, 0, planes0[0], vec)
+        unit = binary("unit", upper, norm[:].unsqueeze(2).to_broadcast([P, 2 * H, 2]))
+        gap = fused("gap", terms[0][:, second, 2], 1.5, terms[0][:, third, 2], ALU.mult, ALU.subtract)
+        sigma = binary("sigma", radius[:, second], inv_radius[:, third])
+        lead = fused("lead", half_sign[:, third], -8.0, radius[:, third], ALU.mult, ALU.mult)
+
+        def newton_sines(n):
+            pair = small("newton_trig%d" % n, 2 * H, 2)
+            size = small("newton_size%d" % n, 2 * H)
+            act.activation(out=size[:], in_=terms[n][:, :, 2], func=ACT.Abs)
+            act.activation(out=pair[:, :, 0], in_=terms[n][:, :, 2], func=ACT.Sin, scale=-1.0)
+            act.activation(out=pair[:, :, 1], in_=size[:], func=ACT.Sin, scale=-1.0, bias=math.pi / 2)
             vec.tensor_tensor(out=terms[n][:, :, 0:2], in0=pair[:], in1=unit[:], op=ALU.mult)
-            filler()
+
+        def newton_sum(n):
             vec.tensor_reduce(out=terms[n + 1][:, :, 2], in_=terms[n][:], op=ALU.add, axis=AXIS_X)
 
-        head_jobs = [k_job(0, 0), q_job(0), k_job(0, 1), k_job(0, 2), k_job(0, 3)]
-        head_tags = ["sum", "sum", "out", "turn", "sum"]
+        head_jobs = [k_job(0, 0), q_job(0, 0, 1), k_job(0, 1), k_job(0, 2), k_job(0, 3), q_job(0, 1, 1)]
+        head_tags = ["sum", "sum", "out", "turn", "sum", "sum"]
 
-        def head_copy(n, engine):
-            return turned_copy(turn(head_jobs[n], head_tags[n]), engine)
+        def head_copy(n):
+            return turned_copy(turn(head_jobs[n], head_tags[n]), act)
 
         def head_quantize(n, grouped):
             quantize(head_jobs[n][1], head_jobs[n][2], grouped[:])
 
-        planes0 = [v_planes_tile(), v_planes_tile()]
-        woven0 = [v_woven_tile(), v_woven_tile()]
-        lead = scaled("lead", b3[:], -4.0)
-        inv_lead = small("inv_lead", H)
-        newton(0, lambda: vec.reciprocal(out=inv_lead[:], in_=lead[:]))
-        staged0 = head_copy(0, act)
-        widen_v(0, 0, 0, planes0[0], vec)
-        newton(1, lambda: head_quantize(0, staged0))
-        staged1 = head_copy(1, act)
-        angle3 = terms[NEWTON_STEPS][:, :, 2]
+        newton_sines(0)
+        staged0 = head_copy(0)
+        sector = affine("sector", gap[:], 2.0 / math.pi, 0.0, dtype=I32)
+        inv_root_sigma = small("inv_root_sigma", H)
+        pool_engine.tensor_tensor(out=inv_root_sigma[:], in0=sigma[:], in1=exponent[:, 0:H], op=ALU.pow)
         widen_v(0, 0, 1, planes0[0], vec)
-        turn_bias = scaled("turn_bias", angle3, 1.0 / (6.0 * math.pi))
-        phase = scaled("phase", angle3, 1.0 / 3.0)
-        staged2 = head_copy(2, vec)
-        head_quantize(1, staged1)
-
-        trig = small("trig", 2, H, 3)
-        for m in range(2):
-            share = (m + 1) / 3.0
-            act.activation(out=trig[:, m, :, 0], in_=angle3, func=ACT.Sin, scale=-share)
-            act.activation(out=trig[:, m, :, 1], in_=angle3, func=ACT.Sin, scale=share, bias=math.pi / 2)
-            act.activation(out=trig[:, m, :, 2], in_=angle3, func=ACT.Sin, scale=share)
-        staged3 = head_copy(3, act)
-        staged4 = head_copy(4, act)
-        head_quantize(2, staged2)
-
-        products = small("products", 2, 2, H, 2)
-        for j in range(2):
-            vec.tensor_tensor(out=products[:, j, :, :, :], in0=ba[:, 0:2, :, :], in1=trig[:, :, :, j:j + 2], op=ALU.mult)
-        head_quantize(3, staged3)
-        rotated = small("rotated", 2, 2, H)
-        vec.tensor_reduce(out=rotated[:].rearrange("p j m h -> p (j m h)"),
-                          in_=products[:].rearrange("p j m h x -> p (j m h) x"), op=ALU.add, axis=AXIS_X)
-        a1, a2 = rotated[:, 0, 0, :], rotated[:, 0, 1, :]
-        b1, b2_plain = rotated[:, 1, 0, :], rotated[:, 1, 1, :]
+        newton_sum(0)
+        thirds = affine("thirds", sector[:], 1.0 / 3.0, 0.0, dtype=I32)
+        halves = affine("halves", sector[:], 0.5, -0.25, dtype=I32)
+        inv_lead = inverse("inv_lead", lead[:])
+        inv_sigma = inverse("inv_sigma", sigma[:])
+        lead_sigma = binary("lead_sigma", lead[:], sigma[:])
+        shift = fused("shift", sector[:], 1.0 / 3.0, thirds[:], ALU.mult, ALU.subtract)
+        odd = fused("odd", halves[:], -2.0, sector[:], ALU.mult, ALU.add)
+        newton_sines(1)
+        staged1 = head_copy(1)
+        staged2 = head_copy(2)
+        head_quantize(0, staged0)
+        newton_sum(1)
+        flip = affine("flip", odd[:], -2.0, 1.0)
         widen_v(0, 0, 2, planes0[0], vec)
-        half_sign2 = affine("half_sign2", b2_plain, 0.0, 0.5, ALU.is_ge, ALU.subtract)
-        rho2 = fused("rho2", a2, -2.0, inv_lead[:], ALU.mult, ALU.mult)
-        linear0 = fused("linear0", b3[:], 3.0, b1, ALU.mult, ALU.add)
-        head_quantize(4, staged4)
-        eps = fused("eps", half_sign2[:], 4.0, half_sign3[:], ALU.mult, ALU.mult)
-        b2 = fused("b2", half_sign2[:], 2.0 * FLOOR, b2_plain, ALU.mult, ALU.add)
+        angle2, angle3 = terms[NEWTON_STEPS][:, second, 2], terms[NEWTON_STEPS][:, third, 2]
+        centre = fused("centre", angle3, 1.0 / (6.0 * math.pi), shift[:], ALU.mult, ALU.add)
+        beta0 = fused("beta0", angle3, -2.0 / 3.0, angle2, ALU.mult, ALU.add)
+        eps = binary("eps", sign23[:], flip[:])
+        head_quantize(1, staged1)
+        turn_bias = fused("turn_bias", eps[:], -0.25, centre[:], ALU.mult, ALU.add)
+        beta = fused("beta", sector[:], -math.pi / 3.0, beta0[:], ALU.mult, ALU.add)
+        signed_lead = binary("signed_lead", lead_sigma[:], eps[:])
+        head_quantize(2, staged2)
+        phase = affine("phase", turn_bias[:], 2.0 * math.pi, 0.0)
+
+        staged3 = head_copy(3)
+        trig = small("trig", H, 3)
+        half_sine_phase = small("half_sine_phase", H)
+        versine = small("versine", H)
+        beta_trig = small("beta_trig", 2, H)
+        act.activation(out=half_sine_phase[:], in_=centre[:], func=ACT.Sin, scale=math.pi)
+        act.activation(out=trig[:, :, 0], in_=centre[:], func=ACT.Sin, scale=-2.0 * math.pi)
+        act.activation(out=trig[:, :, 2], in_=centre[:], func=ACT.Sin, scale=2.0 * math.pi)
+        act.activation(out=beta_trig[:, 0, :], in_=beta[:], func=ACT.Sin)
+        act.activation(out=beta_trig[:, 1, :], in_=beta[:], func=ACT.Sin, bias=math.pi / 2)
+        act.activation(out=versine[:], in_=half_sine_phase[:], func=ACT.Square, scale=math.sqrt(2.0))
+        staged4 = head_copy(4)
+        act.activation(out=trig[:, :, 1], in_=versine[:], func=ACT.Identity, scale=-1.0, bias=1.0)
+        staged5 = head_copy(5)
+
         widen_v(0, 0, 3, planes0[0], vec)
-        eps_b2 = mul("eps_b2", eps[:], b2[:])
-        psi = affine("psi", eps[:], -math.pi / 4, math.pi / 4, ALU.mult, ALU.add)
-        eps_a1 = mul("eps_a1", eps[:], a1)
-        inv_b2 = small("inv_b2", H)
-        vec.reciprocal(out=inv_b2[:], in_=b2[:])
+        both = binary("both", phase[:], beta[:], ALU.add)
+        head_quantize(3, staged3)
+        half_bias = affine("half_bias", both[:], 0.5, math.pi / 4)
+        inv_cos = inverse("inv_cos", beta_trig[:, 1, :])
+        const0 = fused("const0", sigma[:], -0.25, beta_trig[:, 0, :], ALU.mult, ALU.mult)
+        coef = {}
+
+        def coefficients(stage):
+            if stage == 0:
+                coef["products"] = small("products", 2, H, 2)
+                for j in range(2):
+                    vec.tensor_tensor(out=coef["products"][:, j, :, :], in0=ba[:, 0:H, :], in1=trig[:, :, j:j + 2], op=ALU.mult)
+            if stage == 1:
+                coef["first"] = small("first", 2, H)
+                vec.tensor_reduce(out=coef["first"][:].rearrange("p j h -> p (j h)"),
+                                  in_=coef["products"][:].rearrange("p j h x -> p (j h) x"), op=ALU.add, axis=AXIS_X)
+            if stage == 2:
+                coef["ratio"] = binary("ratio", coef["first"][:], inv_lead[:].unsqueeze(1).to_broadcast([P, 2, H]))
+            if stage == 3:
+                coef["q"] = binary("q_coef", coef["ratio"][:, 0, :], inv_cos[:])
+                coef["linear0"] = fused("linear0", sigma[:], -0.5, coef["ratio"][:, 1, :], ALU.mult, ALU.add)
+            if stage == 4:
+                coef["rho"] = fused("rho", coef["q"][:], -2.0, inv_sigma[:], ALU.mult, ALU.mult)
+                coef["linear1"] = binary("linear1", coef["q"][:], beta_trig[:, 0, :])
+                coef["const1"] = binary("const1", coef["q"][:], const0[:], ALU.add)
+            if stage == 5:
+                coef["linear2"] = fused("linear2", coef["linear0"][:], -0.75, coef["linear1"][:], ALU.add, ALU.add)
+                coef["kappa"] = binary("kappa", coef["const1"][:], inv_sigma[:])
+            if stage == 6:
+                coef["rho1"] = binary("rho1", coef["linear2"][:], inv_sigma[:])
+                for h in range(H):
+                    rows = slice(h * PASSES, (h + 1) * PASSES)
+                    vec.tensor_scalar(out=gain_lead[:, rows, :], in0=gain_sb[:, rows, :], scalar1=signed_lead[:, h:h + 1], scalar2=None, op0=ALU.mult)
+
         gain_lead = small("gain_lead", H * PASSES, PACK)
-        for h in range(H):
-            rows = slice(h * PASSES, (h + 1) * PASSES)
-            vec.tensor_scalar(out=gain_lead[:, rows, :], in0=gain_sb[:, rows, :], scalar1=lead[:, h:h + 1], scalar2=None, op0=ALU.mult)
-        sigma = fused("sigma", eps_b2[:], -4.0, inv_lead[:], ALU.mult, ALU.mult)
-        half_bias = fused("half_bias", phase[:], 0.5, psi[:], ALU.mult, ALU.add)
-        linear1 = fused("linear1", eps_b2[:], 2.0, linear0[:], ALU.mult, ALU.add)
-        const0 = small("const0", H)
-        vec.tensor_tensor(out=const0[:], in0=eps_a1[:], in1=a2, op=ALU.add)
-        rho = fused("rho", a1, 0.5, inv_b2[:], ALU.mult, ALU.mult)
-        root_sigma = small("root_sigma", H)
-        pool_engine.tensor_tensor(out=root_sigma[:], in0=sigma[:], in1=exponent[:, 1, :], op=ALU.pow)
-        rho1 = mul("rho1", linear1[:], inv_lead[:])
-        kappa = mul("kappa", const0[:], inv_lead[:])
 
         def wide(name, dtype=F32, bufs=2):
             return work.tile([P, TK], dtype, name=name, bufs=bufs, align_bytes=64)
@@ -287,52 +316,44 @@ def tile_fourierkolmogorovarnoldattention_kernel(tc, q, k, v_bytes, v_scale, ca,
             h = i // Q_TILES
             return tile_[:, h:h + 1]
 
-        def scores(i):
+        WHOLE = slice(0, TK)
+        HALVES = [slice(c * K_PASS, (c + 1) * K_PASS) for c in range(PASSES)]
+
+        def slot(i, name, dtype=F32, bufs=2, width=TK):
+            if name not in st[i]:
+                st[i][name] = work.tile([P, width], dtype, name=name, bufs=bufs, align_bytes=64)
+            return st[i][name]
+
+        def scores(i, c):
             h = i // Q_TILES
             cols = slice((i % 2) * P, (i % 2 + 1) * P)
-            st[i]["score"] = []
-            for c in range(PASSES):
-                bank = psum.tile([P, K_PASS], F32, name="score_bank", tag="score", bufs=BANKS["score"])
-                pe.matmul_mx(out=bank[:], lhsT=q_codes[i // 2][:, cols].bitcast(FP8X4), lhsT_scale=q_scales[i // 2][:, cols],
-                             rhs=k_codes[h][c][:].bitcast(FP8X4), rhs_scale=k_scales[h][c][:], start=True, stop=True)
-                st[i]["score"].append(bank)
+            bank = psum.tile([P, K_PASS], F32, name="score_bank", tag="score", bufs=BANKS["score"])
+            pe.matmul_mx(out=bank[:], lhsT=q_codes[i // 2][:, cols].bitcast(FP8X4), lhsT_scale=q_scales[i // 2][:, cols],
+                         rhs=k_codes[h][c][:].bitcast(FP8X4), rhs_scale=k_scales[h][c][:], start=True, stop=True)
+            st[i].setdefault("score", []).append(bank)
 
-        def turns(i, c):
-            if c == 0:
-                st[i]["u"] = wide("turns", bufs=3)
-            act.activation(out=st[i]["u"][:, c * K_PASS:(c + 1) * K_PASS], in_=st[i]["score"][c][:], func=ACT.Identity,
-                           scale=1.0 / (2.0 * math.pi * math.sqrt(E)), bias=head_col(turn_bias, i))
+        def whole(i, c):
+            n = slot(i, "n%d" % c, I32, width=K_PASS)
+            vec.tensor_scalar(out=n[:], in0=st[i]["score"][c][:], scalar1=1.0 / (2.0 * math.pi * math.sqrt(E)),
+                              scalar2=head_col(turn_bias, i), op0=ALU.mult, op1=ALU.add)
 
-        def whole(i, home, engine):
-            n = home[:].bitcast(I32)
-            if engine is vec:
-                vec.tensor_copy(out=n, in_=st[i]["u"][:])
-            else:
-                pool_engine.tensor_scalar(out=n, in0=st[i]["u"][:], scalar1=1.0, scalar2=0.0, op0=ALU.mult, op1=ALU.add)
-            st[i]["n"] = n
+        def rest(i, c):
+            vec.scalar_tensor_tensor(out=slot(i, "rest", bufs=3)[:, HALVES[c]], in0=st[i]["n%d" % c][:], scalar=-2.0 * math.pi * math.sqrt(E),
+                                     in1=st[i]["score"][c][:], op0=ALU.mult, op1=ALU.add)
 
-        def rest(i):
-            r = wide("rest", bufs=3)
-            for c in range(PASSES):
-                cols = slice(c * K_PASS, (c + 1) * K_PASS)
-                vec.scalar_tensor_tensor(out=r[:, cols], in0=st[i]["n"][:, cols], scalar=-2.0 * math.pi * math.sqrt(E),
-                                         in1=st[i]["score"][c][:], op0=ALU.mult, op1=ALU.add)
-            st[i]["r"] = r
+        def folded(i, cols=WHOLE):
+            act.activation(out=slot(i, "folded")[:, cols], in_=st[i]["rest"][:, cols], func=ACT.Abs,
+                           scale=1.0 / math.sqrt(E), bias=head_col(phase, i))
 
-        def sine(i):
-            x = wide("x", bufs=3)
-            act.activation(out=x[:], in_=st[i]["r"][:], func=ACT.Sin, scale=1.0 / math.sqrt(E), bias=head_col(phase, i))
-            st[i]["x"] = x
+        def sine(i, cols=WHOLE):
+            act.activation(out=slot(i, "x", bufs=3)[:, cols], in_=st[i]["folded"][:, cols], func=ACT.Sin, scale=-1.0, bias=math.pi / 2)
 
-        def half_sine(i):
-            half = wide("half")
-            act.activation(out=half[:], in_=st[i]["r"][:], func=ACT.Sin, scale=0.5 / math.sqrt(E), bias=head_col(half_bias, i))
-            st[i]["half"] = half
+        def half_sine(i, cols=WHOLE):
+            act.activation(out=slot(i, "half", bufs=3)[:, cols], in_=st[i]["rest"][:, cols], func=ACT.Sin,
+                           scale=0.5 / math.sqrt(E), bias=head_col(half_bias, i))
 
-        def squared(i):
-            w = wide("w", bufs=3)
-            act.activation(out=w[:], in_=st[i]["half"][:], func=ACT.Square, scale=head_col(root_sigma, i))
-            st[i]["w"] = w
+        def squared(i, cols=WHOLE):
+            act.activation(out=slot(i, "square", bufs=3)[:, cols], in_=st[i]["x"][:, cols], func=ACT.Square, scale=head_col(inv_root_sigma, i))
 
         def shifted_product(i, name, a, shift, b, cols):
             if name not in st[i]:
@@ -341,9 +362,16 @@ def tile_fourierkolmogorovarnoldattention_kernel(tc, q, k, v_bytes, v_scale, ca,
                                      in1=st[i][b][:, cols], op0=ALU.add, op1=ALU.mult)
 
         def products_of(i, cols):
-            shifted_product(i, "square", "x", rho2, "x", cols)
-            shifted_product(i, "mixed", "x", rho, "w", cols)
-            shifted_product(i, "cubic", "square", rho1, "x", cols)
+            shifted_product(i, "cubic", "square", coef["rho1"], "x", cols)
+            shifted_product(i, "mixed", "x", coef["rho"], "w", cols)
+
+        def square_half(i, engine, cols=WHOLE):
+            if "w" not in st[i]:
+                st[i]["w"] = wide("w_late") if i >= last - 1 else wide("w", bufs=1)
+            if engine is act:
+                act.activation(out=st[i]["w"][:, cols], in_=st[i]["half"][:, cols], func=ACT.Square)
+            else:
+                pool_engine.tensor_tensor(out=st[i]["w"][:], in0=st[i]["half"][:], in1=st[i]["half"][:], op=ALU.mult)
 
         def sum_turned(i, c, tag):
             bank = psum.tile([P, PACK, P], F32, name="sum_bank", tag=tag, bufs=BANKS[tag])
@@ -362,12 +390,12 @@ def tile_fourierkolmogorovarnoldattention_kernel(tc, q, k, v_bytes, v_scale, ca,
                 row = h * PASSES + c
                 vec.scalar_tensor_tensor(
                     out=ag[:, c * K_PASS:(c + 1) * K_PASS].rearrange("p (r t) -> p r t", t=PACK),
-                    in0=st[i]["sum"][c][:].rearrange("p t r -> p r t"), scalar=head_col(kappa, i),
+                    in0=st[i]["sum"][c][:].rearrange("p t r -> p r t"), scalar=head_col(coef["kappa"], i),
                     in1=gain_lead[:, row:row + 1, :].to_broadcast([P, P, PACK]), op0=ALU.add, op1=ALU.mult)
 
         def quantize_ag(i, parts=1):
-            codes = work.tile([P, PASSES * P], U32, name="ag_codes", align_bytes=64, bufs=6)
-            scales = work.tile([P, PASSES * P], U8, name="ag_scales", align_bytes=64, bufs=6)
+            codes = work.tile([P, PASSES * P], U32, name="ag_codes", align_bytes=64, bufs=10)
+            scales = work.tile([P, PASSES * P], U8, name="ag_scales", align_bytes=64, bufs=10)
             width = PASSES * P // parts
             for j in range(parts):
                 cols = slice(j * width, (j + 1) * width)
@@ -390,125 +418,166 @@ def tile_fourierkolmogorovarnoldattention_kernel(tc, q, k, v_bytes, v_scale, ca,
             dma.dma_start(out=out[h, row * P:(row + 1) * P, :], in_=result[:])
 
         loop_jobs = [q_job(3)] + [k_job(1, j) for j in range(2 * PASSES)] + [q_job(j) for j in range(4, TILES // 2)]
-        JOB_START = 1
+        JOB_START = 2
         job_bank = {}
         job_staged = {}
-        planes1 = []
-        woven1 = []
-        WIDEN_START = 3
-        WEAVE_START = WIDEN_START + PASSES * PACK
-        V1_READY = WEAVE_START + 2 * PASSES + 1
-        mix_step = {i: i + 5 for i in range(Q_TILES)}
-        for i in range(Q_TILES, TILES):
-            mix_step[i] = max(i + 5, V1_READY + (i - Q_TILES) // 2)
+        v_blocks = [(0, 1), (1, 0), (1, 1)]
+        v_tiles = {}
+        V_START = 4
+        V_WIDENS = 1
+        V_UNITS = 2 * PACK
+        V_STEPS = 10
+        CATCH_UP = 13
+
+        def v_unit(n, engine):
+            block, unit_index = divmod(n, V_UNITS)
+            if (engine is vec) != (unit_index < PACK and block < V_WIDENS):
+                return
+            h, c = v_blocks[block]
+            if unit_index == 0:
+                v_tiles[block] = (v_planes_tile(), v_woven_tile())
+            planes, woven = v_tiles[block]
+            if unit_index < PACK:
+                widen_v(h, c, unit_index, planes, engine)
+            else:
+                part = unit_index - PACK
+                interleave_v(planes, woven, slice(part * DV // PACK, (part + 1) * DV // PACK), act)
 
         def live(i):
             return 0 <= i < TILES
 
         last = TILES - 1
-        scores(0)
-        scores(1)
+        waiting = list(range(last))
+        def unit_step(n):
+            return V_START + n * V_STEPS // (len(v_blocks) * V_UNITS)
+
+        v_done = [unit_step((block + 1) * V_UNITS - 1) + 1 for block in range(len(v_blocks))]
+
+        mixed_tiles = []
+
+        def mix_next(s):
+            if waiting and s >= max(waiting[0] + 5, v_done[2 * (waiting[0] // Q_TILES)]):
+                mixed_tiles.append(waiting.pop(0))
+                mix_values(mixed_tiles[-1], "out")
+
+        def store_next():
+            if mixed_tiles:
+                store(mixed_tiles.pop(0))
+
+        scores(0, 0)
+        whole(0, 0)
+        head_quantize(4, staged4)
+        rest(0, 0)
+        head_quantize(5, staged5)
+        scores(0, 1)
+        for c in range(PASSES):
+            scores(1, c)
         bank_q1 = turn(q_job(1), "sum")
         bank_q2 = turn(q_job(2), "sum")
-        job_bank[JOB_START] = turn(loop_jobs[0], "turn")
-        for i in range(2):
-            for c in range(PASSES):
-                turns(i, c)
-        staged_q1 = turned_copy(bank_q1, act)
-        whole(0, wide("square"), vec)
-        interleave_v(planes0[0], woven0[0], slice(0, DV // 2), vec)
-        rest(0)
-        whole(1, wide("square"), vec)
+        coefficients(0)
+        whole(0, 1)
+        coefficients(1)
+        interleave_v(planes0[0], woven0[0], slice(0, DV // 4), vec)
+        rest(0, 1)
+        for cols in HALVES:
+            folded(0, cols)
+            half_sine(0, cols)
+            sine(0, cols)
+            square_half(0, act, cols)
+            squared(0, cols)
+        coefficients(2)
+        whole(1, 0)
+        coefficients(3)
+        whole(1, 1)
+        coefficients(4)
+        rest(1, 0)
+        staged_q1 = turned_copy(bank_q1, vec)
+        coefficients(5)
+        rest(1, 1)
+        coefficients(6)
         quantize(q_job(1)[1], q_job(1)[2], staged_q1[:])
-        rest(1)
-        for s in range(2, TILES + 3):
-            mixes = [i for i in range(last - 2) if mix_step[i] == s]
-            if live(s):
-                scores(s)
-            if mixes:
-                mix_values(mixes[0])
-            if live(s - 4) and s - 4 != last:
-                for c in range(EARLY, PASSES):
-                    sum_turned(s - 4, c, "sum")
-            if s - 1 in job_bank:
+        interleave_v(planes0[0], woven0[0], slice(DV // 4, DV), vec)
+        job_bank[JOB_START] = turn(loop_jobs[0], "turn")
+        for c in range(PASSES):
+            scores(2, c)
+        for s in range(3, TILES + 1):
+            folded(s - 2)
+            half_sine(s - 2)
+            sine(s - 2)
+            if s - 1 in job_bank and s != 4:
                 job_staged[s - 1] = turned_copy(job_bank[s - 1], act)
-            if s - JOB_START < len(loop_jobs):
-                job_bank[s] = turn(loop_jobs[s - JOB_START], "turn")
-            if live(s - 2):
-                sine(s - 2)
-            if s == 2:
-                half_sine(0)
-            if live(s):
-                turns(s, 0)
-            if s == 2:
-                squared(0)
-            elif live(s - 2):
-                half_sine(s - 2)
-            if live(s):
-                turns(s, 1)
-            elif mixes:
-                store(mixes[0])
-                mixes = mixes[1:]
-                if mixes:
-                    mix_values(mixes[0])
-            if live(s - 2) and s > 2:
-                squared(s - 2)
-            if mixes:
-                store(mixes[0])
-            if 0 <= s - WIDEN_START < PASSES * PACK:
-                c, t = divmod(s - WIDEN_START, PACK)
-                if t == 0:
-                    planes1.append(v_planes_tile())
-                widen_v(1, c, t, planes1[c], act)
-            if 0 <= s - WEAVE_START < 2 * PASSES:
-                c, part = divmod(s - WEAVE_START, 2)
-                if part == 0:
-                    woven1.append(v_woven_tile())
-                interleave_v(planes1[c], woven1[c], slice(part * DV // 2, (part + 1) * DV // 2), act)
-            if s == 2:
-                interleave_v(planes0[0], woven0[0], slice(DV // 2, DV), vec)
-                staged_q2 = turned_copy(bank_q2, vec)
-                for t in range(PACK):
-                    widen_v(0, 1, t, planes0[1], vec)
-                quantize(v_codes[0][0][:], v_scales[0][0][:], woven0[0][:])
-                interleave_v(planes0[1], woven0[1], slice(0, DV), vec)
-                quantize(q_job(2)[1], q_job(2)[2], staged_q2[:])
-            if s - 3 == last:
-                for c in range(PASSES):
-                    products_of(last, slice(c * K_PASS, (c + 1) * K_PASS))
-                    sum_turned(last, c, "score")
-                    if c == 0:
-                        quantize_ag(last - 2)
-            elif live(s - 3):
-                products_of(s - 3, slice(0, TK))
-            if live(s) and live(s - 3):
-                whole(s, st[s - 3]["square"], pool_engine)
-            if live(s - 4):
-                gained(s - 4)
-            if live(s - 3) and s - 3 != last:
-                for c in range(EARLY):
-                    sum_turned(s - 3, c, "sum")
-            if live(s - 1) and s > 2:
-                rest(s - 1)
+            else:
+                store_next()
+            squared(s - 2)
+            if s - 2 == last - 1:
+                square_half(s - 2, act)
+            store_next()
+            for n in range(len(v_blocks) * V_UNITS):
+                if unit_step(n) == s:
+                    v_unit(n, act)
             if s == 3:
-                quantize(v_codes[0][1][:], v_scales[0][1][:], woven0[1][:])
-            if live(s - 4) and live(s - 1):
-                quantize_ag(s - 4)
+                staged_q2 = turned_copy(bank_q2, vec)
+            else:
+                products_of(s - 4, WHOLE)
+                square_half(s - 3, pool_engine)
+            if s == 4:
+                job_staged[s - 1] = turned_copy(job_bank[s - 1], vec)
+            if s >= 5:
+                gained(s - 5)
+            for c in range(PASSES):
+                whole(s - 1, c)
+            for c in range(PASSES):
+                rest(s - 1, c)
+            if s == 3:
+                quantize(v_codes[0][0][:], v_scales[0][0][:], woven0[0][:])
+                quantize(q_job(2)[1], q_job(2)[2], staged_q2[:])
+            else:
+                for c in range(PASSES):
+                    sum_turned(s - 4, c, "sum")
+            if s >= 5:
+                quantize_ag(s - 5)
             if s - 1 in job_staged:
                 quantize(loop_jobs[s - 1 - JOB_START][1], loop_jobs[s - 1 - JOB_START][2], job_staged[s - 1][:])
-            if s - WEAVE_START in (2, 4):
-                c = (s - WEAVE_START) // 2 - 1
-                quantize(v_codes[1][c][:], v_scales[1][c][:], woven1[c][:])
-            if s < 3:
-                whole(s, wide("square"), vec)
-        mix_values(last - 2, "turn")
+            for block in range(len(v_blocks)):
+                if s == v_done[block]:
+                    h, c = v_blocks[block]
+                    quantize(v_codes[h][c][:], v_scales[h][c][:], v_tiles[block][1][:])
+            for n in range(len(v_blocks) * V_UNITS):
+                if unit_step(n) == s + 1:
+                    v_unit(n, vec)
+            if s < TILES:
+                for c in range(PASSES):
+                    scores(s, c)
+            if s - JOB_START < len(loop_jobs):
+                job_bank[s] = turn(loop_jobs[s - JOB_START], "turn")
+            mix_next(s)
+            if s >= CATCH_UP:
+                mix_next(s)
+        for cols in HALVES:
+            folded(last, cols)
+            half_sine(last, cols)
+            sine(last, cols)
+            square_half(last, act, cols)
+            squared(last, cols)
+        drain_tags = {last - 2: ["score", "score"], last - 1: ["sum", "sum"], last: ["score", "score"]}
+        for i in range(last - 2, TILES):
+            for c in range(PASSES):
+                products_of(i, HALVES[c])
+                sum_turned(i, c, drain_tags[i][c])
+                if c == 0 and i > last - 2:
+                    quantize_ag(i - 2)
+            while waiting and waiting[0] <= i - 2:
+                store_next()
+                mix_next(TILES + 5)
+            gained(i - 1)
         gained(last, [0])
         quantize_ag(last - 1)
         gained(last, [1])
-        store(last - 2)
-        mix_values(last - 1)
+        store_next()
+        mix_next(TILES + 5)
         quantize_ag(last, PASSES)
-        store(last - 1)
+        store_next()
+        store_next()
         h, row = divmod(last, Q_TILES)
         for part in range(2):
             cols = slice(part * DV // 2, (part + 1) * DV // 2)

import math
from contextlib import ExitStack

import concourse.mybir as mybir
from concourse.masks import make_identity

H, TQ, TK, E, DV, HARMONICS = 2, 1024, 1024, 512, 512, 3
FLOPS = 2 * H * TQ * TK * E + 2 * H * TQ * TK * DV

F32 = mybir.dt.float32
BF16 = mybir.dt.bfloat16
I32 = mybir.dt.int32
U32 = mybir.dt.uint32
U8 = mybir.dt.uint8
FP8 = mybir.dt.float8_e4m3fn
FP8X4 = mybir.dt.float8_e4m3fn_x4
ALU = mybir.AluOpType
ACT = mybir.ActivationFunctionType
AXIS_X = mybir.AxisListType.X

P = 128
PACK = 4
K_PASS = P * PACK
PASSES = TK // K_PASS
Q_TILES = TQ // P
TILES = H * Q_TILES
NEWTON_STEPS = 2
FLOOR = 2.0 ** -60
BANKS = {"score": 3, "sum": 2, "out": 2, "turn": 1}


def tile_fourierkolmogorovarnoldattention_kernel(tc, q, k, v_bytes, v_scale, ca, cb, g, out):
    nc = tc.nc
    vec, act, pe, pool_engine, dma = nc.vector, nc.scalar, nc.tensor, nc.gpsimd, nc.sync

    with ExitStack() as ctx:
        keep = ctx.enter_context(tc.tile_pool(name="keep", bufs=1))
        work = ctx.enter_context(tc.tile_pool(name="work", bufs=2))
        psum = ctx.enter_context(tc.psum_pool(name="psum", bufs=2))
        ctx.enter_context(tc.manual_schedule())

        def kept(name, shape, dtype):
            return keep.tile(shape, dtype, name=name, align_bytes=64)

        ca_sb = kept("ca_sb", [P, H * HARMONICS], BF16)
        cb_sb = kept("cb_sb", [P, H * HARMONICS], BF16)
        k_rows = [[kept("k_rows%d%d" % (h, j), [P, 2 * E], BF16) for j in range(2 * PASSES)] for h in range(H)]
        q_rows = [kept("q_rows%d" % j, [P, 2 * E], BF16) for j in range(TILES // 2)]
        v_raw = [[kept("v_raw%d%d" % (h, c), [P, PACK * DV], U8) for c in range(PASSES)] for h in range(H)]
        v_scale_sb = kept("v_scale_sb", [P, PASSES, PACK], F32)
        gain_sb = kept("gain_sb", [P, H * PASSES, PACK], BF16)

        def load_k(h, j):
            c, half = divmod(j, 2)
            rows = k[h, c * K_PASS:(c + 1) * K_PASS, :].rearrange("(m t) e -> m (t e)", t=PACK)
            dma.dma_start(out=k_rows[h][j][:], in_=rows[:, half * 2 * E:(half + 1) * 2 * E])

        def load_q(j):
            h, first = divmod(2 * j, Q_TILES)
            dma.dma_start(out=q_rows[j][:].rearrange("p (i e) -> p i e", i=2),
                          in_=q[h, first * P:(first + 2) * P, :].rearrange("(i p) e -> p i e", p=P))

        def load_v(h, c):
            dma.dma_start(out=v_raw[h][c][:], in_=v_bytes[h, c * K_PASS:(c + 1) * K_PASS, :].rearrange("(p t) n -> p (t n)", t=PACK))

        act.dma_start(out=ca_sb[:], in_=ca.rearrange("h m -> (h m)").partition_broadcast(P))
        act.dma_start(out=cb_sb[:], in_=cb.rearrange("h m -> (h m)").partition_broadcast(P))
        load_k(0, 0)
        dma.dma_start(out=v_scale_sb[:], in_=v_scale.rearrange("o (c p t) x -> p (o c) (t x)", p=P, t=PACK))
        load_v(0, 0)
        load_q(0)
        load_k(0, 1)
        load_k(0, 2)
        load_k(0, 3)
        load_q(1)
        load_v(0, 1)
        dma.dma_start(out=gain_sb[:], in_=g.rearrange("h (c p t) -> p (h c) t", p=P, t=PACK))
        load_q(2)
        load_q(3)
        for j in range(2 * PASSES):
            load_k(1, j)
        for j in range(4, TILES // 2):
            load_q(j)
        for c in range(PASSES):
            load_v(1, c)

        ident = kept("ident", [P, P], F32)
        make_identity(nc, ident[:])
        exponent = kept("exponent", [P, 2 * H], F32)
        pool_engine.memset(exponent[:], -0.5)
        warm = kept("warm", [P, 2], F32)
        vec.memset(warm[:, 0:1], 0.0)
        act.activation(out=warm[:, 1:2], in_=warm[:, 0:1], func=ACT.Sin)

        k_codes = [[kept("k_codes%d%d" % (h, c), [P, K_PASS], U32) for c in range(PASSES)] for h in range(H)]
        k_scales = [[kept("k_scales%d%d" % (h, c), [P, K_PASS], U8) for c in range(PASSES)] for h in range(H)]
        q_codes = [kept("q_codes%d" % j, [P, 2 * P], U32) for j in range(TILES // 2)]
        q_scales = [kept("q_scales%d" % j, [P, 2 * P], U8) for j in range(TILES // 2)]
        v_codes = [[kept("v_codes%d%d" % (h, c), [P, DV], U32) for c in range(PASSES)] for h in range(H)]
        v_scales = [[kept("v_scales%d%d" % (h, c), [P, DV], U8) for c in range(PASSES)] for h in range(H)]

        def k_job(h, j):
            c, half = divmod(j, 2)
            cols = slice(half * 2 * P, (half + 1) * 2 * P)
            return (k_rows[h][j][:], k_codes[h][c][:, cols], k_scales[h][c][:, cols])

        def q_job(j, first=0, count=2):
            cols = slice(first * P, (first + count) * P)
            return (q_rows[j][:, first * E:(first + count) * E], q_codes[j][:, cols], q_scales[j][:, cols])

        def turn(job, tag):
            words = job[0].bitcast(F32)
            count = words.shape[1] // (E // 2)
            bank = psum.tile([P, count, 2, P], F32, name="turn_bank", tag=tag, bufs=BANKS[tag])
            for i in range(count):
                for u in range(2):
                    pe.transpose(bank[:, i, u, :], words[:, i * (E // 2) + u:(i + 1) * (E // 2):2], ident[:])
            return bank

        def turned_copy(bank, engine):
            count = bank[:].shape[1]
            grouped = work.tile([P, count * P * PACK], BF16, name="grouped", align_bytes=64, bufs=5)
            dst = grouped[:].bitcast(F32).rearrange("p (i r u) -> p i r u", i=count, u=2)
            src = bank[:].rearrange("p i u r -> p i r u")
            if engine is act:
                act.copy(out=dst, in_=src)
            else:
                vec.tensor_copy(out=dst, in_=src)
            return grouped

        def quantize(codes, scales, values):
            vec.quantize_mx(out=codes.bitcast(FP8X4), scales=scales, in_=values)

        def v_planes_tile():
            return work.tile([P, PACK, DV], BF16, name="v_planes", align_bytes=64)

        def v_woven_tile():
            return work.tile([P, DV * PACK], BF16, name="v_woven", align_bytes=64)

        def widen_v(h, c, t, planes, engine):
            src = v_raw[h][c][:, t * DV:(t + 1) * DV].bitcast(FP8)
            if engine is act:
                act.activation(out=planes[:, t, :], in_=src, func=ACT.Copy, scale=v_scale_sb[:, c, t:t + 1])
            else:
                vec.tensor_scalar(out=planes[:, t, :], in0=src, scalar1=v_scale_sb[:, c, t:t + 1], scalar2=None, op0=ALU.mult)

        def interleave_v(planes, woven, cols, engine):
            dst = woven[:].rearrange("p (n t) -> p n t", t=PACK)[:, cols, :].rearrange("p (c i) t -> p c t i", i=4)
            src = planes[:, :, cols].rearrange("p t (c i) -> p c t i", i=4)
            if engine is act:
                act.copy(out=dst, in_=src)
            else:
                vec.tensor_copy(out=dst, in_=src)

        def small(name, *shape, dtype=F32):
            return kept(name, [P] + list(shape), dtype)

        def binary(name, a, b, op=ALU.mult):
            o = small(name, *a.shape[1:])
            vec.tensor_tensor(out=o[:], in0=a, in1=b, op=op)
            return o

        def fused(name, a, scalar, b, op0, op1):
            o = small(name, *a.shape[1:])
            vec.scalar_tensor_tensor(out=o[:], in0=a, scalar=scalar, in1=b, op0=op0, op1=op1)
            return o

        def affine(name, a, s1, s2, op0=ALU.mult, op1=ALU.add, dtype=F32):
            o = small(name, *a.shape[1:], dtype=dtype)
            vec.tensor_scalar(out=o[:], in0=a, scalar1=s1, scalar2=s2, op0=op0, op1=op1)
            return o

        def inverse(name, a):
            o = small(name, *a.shape[1:])
            vec.reciprocal(out=o[:], in_=a)
            return o

        second, third = slice(0, H), slice(H, 2 * H)
        ba = small("ba", HARMONICS * H, 2)
        vec.tensor_copy(out=ba[:, :, 0].rearrange("p (m h) -> p m h", h=H), in_=cb_sb[:].rearrange("p (h m) -> p m h", h=H))
        vec.tensor_copy(out=ba[:, :, 1].rearrange("p (m h) -> p m h", h=H), in_=ca_sb[:].rearrange("p (h m) -> p m h", h=H))
        upper = ba[:, H:, :]
        squares = binary("squares", upper, upper)
        taxi = small("taxi", 2 * H)
        vec.tensor_reduce(out=taxi[:], in_=upper, op=ALU.add, axis=AXIS_X, apply_absolute_value=True)
        half_sign = affine("half_sign", upper[:, :, 0], 0.0, 0.5, ALU.is_ge, ALU.subtract)
        radius2 = fused("radius2", squares[:, :, 0], FLOOR * FLOOR, squares[:, :, 1], ALU.add, ALU.add)
        inv_radius = small("inv_radius", 2 * H)
        pool_engine.tensor_tensor(out=inv_radius[:], in0=radius2[:], in1=exponent[:], op=ALU.pow)
        taxi_safe = affine("taxi_safe", taxi[:], FLOOR, 1.0 / math.pi, ALU.add, ALU.mult)
        signed_a = binary("signed_a", upper[:, :, 1], half_sign[:])
        inv_taxi = inverse("inv_taxi", taxi_safe[:])
        sign23 = fused("sign23", half_sign[:, second], 4.0, half_sign[:, third], ALU.mult, ALU.mult)
        terms = [small("terms%d" % n, 2 * H, 3) for n in range(NEWTON_STEPS + 1)]
        vec.tensor_tensor(out=terms[0][:, :, 2], in0=signed_a[:], in1=inv_taxi[:], op=ALU.mult)
        planes0 = [v_planes_tile()]
        woven0 = [v_woven_tile()]
        norm = fused("norm", half_sign[:], 2.0, inv_radius[:], ALU.mult, ALU.mult)
        radius = binary("radius", radius2[:], inv_radius[:])
        widen_v(0, 0, 0, planes0[0], vec)
        unit = binary("unit", upper, norm[:].unsqueeze(2).to_broadcast([P, 2 * H, 2]))
        gap = fused("gap", terms[0][:, second, 2], 1.5, terms[0][:, third, 2], ALU.mult, ALU.subtract)
        sigma = binary("sigma", radius[:, second], inv_radius[:, third])
        lead = fused("lead", half_sign[:, third], -8.0, radius[:, third], ALU.mult, ALU.mult)

        def newton_sines(n):
            pair = small("newton_trig%d" % n, 2 * H, 2)
            size = small("newton_size%d" % n, 2 * H)
            act.activation(out=size[:], in_=terms[n][:, :, 2], func=ACT.Abs)
            act.activation(out=pair[:, :, 0], in_=terms[n][:, :, 2], func=ACT.Sin, scale=-1.0)
            act.activation(out=pair[:, :, 1], in_=size[:], func=ACT.Sin, scale=-1.0, bias=math.pi / 2)
            vec.tensor_tensor(out=terms[n][:, :, 0:2], in0=pair[:], in1=unit[:], op=ALU.mult)

        def newton_sum(n):
            vec.tensor_reduce(out=terms[n + 1][:, :, 2], in_=terms[n][:], op=ALU.add, axis=AXIS_X)

        head_jobs = [k_job(0, 0), q_job(0, 0, 1), k_job(0, 1), k_job(0, 2), k_job(0, 3), q_job(0, 1, 1)]
        head_tags = ["sum", "sum", "out", "turn", "sum", "sum"]

        def head_copy(n):
            return turned_copy(turn(head_jobs[n], head_tags[n]), act)

        def head_quantize(n, grouped):
            quantize(head_jobs[n][1], head_jobs[n][2], grouped[:])

        newton_sines(0)
        staged0 = head_copy(0)
        sector = affine("sector", gap[:], 2.0 / math.pi, 0.0, dtype=I32)
        inv_root_sigma = small("inv_root_sigma", H)
        pool_engine.tensor_tensor(out=inv_root_sigma[:], in0=sigma[:], in1=exponent[:, 0:H], op=ALU.pow)
        widen_v(0, 0, 1, planes0[0], vec)
        newton_sum(0)
        thirds = affine("thirds", sector[:], 1.0 / 3.0, 0.0, dtype=I32)
        halves = affine("halves", sector[:], 0.5, -0.25, dtype=I32)
        inv_lead = inverse("inv_lead", lead[:])
        inv_sigma = inverse("inv_sigma", sigma[:])
        lead_sigma = binary("lead_sigma", lead[:], sigma[:])
        shift = fused("shift", sector[:], 1.0 / 3.0, thirds[:], ALU.mult, ALU.subtract)
        odd = fused("odd", halves[:], -2.0, sector[:], ALU.mult, ALU.add)
        newton_sines(1)
        staged1 = head_copy(1)
        staged2 = head_copy(2)
        head_quantize(0, staged0)
        newton_sum(1)
        flip = affine("flip", odd[:], -2.0, 1.0)
        widen_v(0, 0, 2, planes0[0], vec)
        angle2, angle3 = terms[NEWTON_STEPS][:, second, 2], terms[NEWTON_STEPS][:, third, 2]
        centre = fused("centre", angle3, 1.0 / (6.0 * math.pi), shift[:], ALU.mult, ALU.add)
        beta0 = fused("beta0", angle3, -2.0 / 3.0, angle2, ALU.mult, ALU.add)
        eps = binary("eps", sign23[:], flip[:])
        head_quantize(1, staged1)
        turn_bias = fused("turn_bias", eps[:], -0.25, centre[:], ALU.mult, ALU.add)
        beta = fused("beta", sector[:], -math.pi / 3.0, beta0[:], ALU.mult, ALU.add)
        signed_lead = binary("signed_lead", lead_sigma[:], eps[:])
        head_quantize(2, staged2)
        phase = affine("phase", turn_bias[:], 2.0 * math.pi, 0.0)

        staged3 = head_copy(3)
        trig = small("trig", H, 3)
        half_sine_phase = small("half_sine_phase", H)
        versine = small("versine", H)
        beta_trig = small("beta_trig", 2, H)
        act.activation(out=half_sine_phase[:], in_=centre[:], func=ACT.Sin, scale=math.pi)
        act.activation(out=trig[:, :, 0], in_=centre[:], func=ACT.Sin, scale=-2.0 * math.pi)
        act.activation(out=trig[:, :, 2], in_=centre[:], func=ACT.Sin, scale=2.0 * math.pi)
        act.activation(out=beta_trig[:, 0, :], in_=beta[:], func=ACT.Sin)
        act.activation(out=beta_trig[:, 1, :], in_=beta[:], func=ACT.Sin, bias=math.pi / 2)
        act.activation(out=versine[:], in_=half_sine_phase[:], func=ACT.Square, scale=math.sqrt(2.0))
        staged4 = head_copy(4)
        act.activation(out=trig[:, :, 1], in_=versine[:], func=ACT.Identity, scale=-1.0, bias=1.0)
        staged5 = head_copy(5)

        widen_v(0, 0, 3, planes0[0], vec)
        both = binary("both", phase[:], beta[:], ALU.add)
        head_quantize(3, staged3)
        half_bias = affine("half_bias", both[:], 0.5, math.pi / 4)
        inv_cos = inverse("inv_cos", beta_trig[:, 1, :])
        const0 = fused("const0", sigma[:], -0.25, beta_trig[:, 0, :], ALU.mult, ALU.mult)
        coef = {}

        def coefficients(stage):
            if stage == 0:
                coef["products"] = small("products", 2, H, 2)
                for j in range(2):
                    vec.tensor_tensor(out=coef["products"][:, j, :, :], in0=ba[:, 0:H, :], in1=trig[:, :, j:j + 2], op=ALU.mult)
            if stage == 1:
                coef["first"] = small("first", 2, H)
                vec.tensor_reduce(out=coef["first"][:].rearrange("p j h -> p (j h)"),
                                  in_=coef["products"][:].rearrange("p j h x -> p (j h) x"), op=ALU.add, axis=AXIS_X)
            if stage == 2:
                coef["ratio"] = binary("ratio", coef["first"][:], inv_lead[:].unsqueeze(1).to_broadcast([P, 2, H]))
            if stage == 3:
                coef["q"] = binary("q_coef", coef["ratio"][:, 0, :], inv_cos[:])
                coef["linear0"] = fused("linear0", sigma[:], -0.5, coef["ratio"][:, 1, :], ALU.mult, ALU.add)
            if stage == 4:
                coef["rho"] = fused("rho", coef["q"][:], -2.0, inv_sigma[:], ALU.mult, ALU.mult)
                coef["linear1"] = binary("linear1", coef["q"][:], beta_trig[:, 0, :])
                coef["const1"] = binary("const1", coef["q"][:], const0[:], ALU.add)
            if stage == 5:
                coef["linear2"] = fused("linear2", coef["linear0"][:], -0.75, coef["linear1"][:], ALU.add, ALU.add)
                coef["kappa"] = binary("kappa", coef["const1"][:], inv_sigma[:])
            if stage == 6:
                coef["rho1"] = binary("rho1", coef["linear2"][:], inv_sigma[:])
                for h in range(H):
                    rows = slice(h * PASSES, (h + 1) * PASSES)
                    vec.tensor_scalar(out=gain_lead[:, rows, :], in0=gain_sb[:, rows, :], scalar1=signed_lead[:, h:h + 1], scalar2=None, op0=ALU.mult)

        gain_lead = small("gain_lead", H * PASSES, PACK)

        def wide(name, dtype=F32, bufs=2):
            return work.tile([P, TK], dtype, name=name, bufs=bufs, align_bytes=64)

        st = [dict() for i in range(TILES)]

        def head_col(tile_, i):
            h = i // Q_TILES
            return tile_[:, h:h + 1]

        WHOLE = slice(0, TK)
        HALVES = [slice(c * K_PASS, (c + 1) * K_PASS) for c in range(PASSES)]

        def slot(i, name, dtype=F32, bufs=2, width=TK):
            if name not in st[i]:
                st[i][name] = work.tile([P, width], dtype, name=name, bufs=bufs, align_bytes=64)
            return st[i][name]

        def scores(i, c):
            h = i // Q_TILES
            cols = slice((i % 2) * P, (i % 2 + 1) * P)
            bank = psum.tile([P, K_PASS], F32, name="score_bank", tag="score", bufs=BANKS["score"])
            pe.matmul_mx(out=bank[:], lhsT=q_codes[i // 2][:, cols].bitcast(FP8X4), lhsT_scale=q_scales[i // 2][:, cols],
                         rhs=k_codes[h][c][:].bitcast(FP8X4), rhs_scale=k_scales[h][c][:], start=True, stop=True)
            st[i].setdefault("score", []).append(bank)

        def whole(i, c):
            n = slot(i, "n%d" % c, I32, width=K_PASS)
            vec.tensor_scalar(out=n[:], in0=st[i]["score"][c][:], scalar1=1.0 / (2.0 * math.pi * math.sqrt(E)),
                              scalar2=head_col(turn_bias, i), op0=ALU.mult, op1=ALU.add)

        def rest(i, c):
            vec.scalar_tensor_tensor(out=slot(i, "rest", bufs=3)[:, HALVES[c]], in0=st[i]["n%d" % c][:], scalar=-2.0 * math.pi * math.sqrt(E),
                                     in1=st[i]["score"][c][:], op0=ALU.mult, op1=ALU.add)

        def folded(i, cols=WHOLE):
            act.activation(out=slot(i, "folded")[:, cols], in_=st[i]["rest"][:, cols], func=ACT.Abs,
                           scale=1.0 / math.sqrt(E), bias=head_col(phase, i))

        def sine(i, cols=WHOLE):
            act.activation(out=slot(i, "x", bufs=3)[:, cols], in_=st[i]["folded"][:, cols], func=ACT.Sin, scale=-1.0, bias=math.pi / 2)

        def half_sine(i, cols=WHOLE):
            act.activation(out=slot(i, "half", bufs=3)[:, cols], in_=st[i]["rest"][:, cols], func=ACT.Sin,
                           scale=0.5 / math.sqrt(E), bias=head_col(half_bias, i))

        def squared(i, cols=WHOLE):
            act.activation(out=slot(i, "square", bufs=3)[:, cols], in_=st[i]["x"][:, cols], func=ACT.Square, scale=head_col(inv_root_sigma, i))

        def shifted_product(i, name, a, shift, b, cols):
            if name not in st[i]:
                st[i][name] = wide(name)
            vec.scalar_tensor_tensor(out=st[i][name][:, cols], in0=st[i][a][:, cols], scalar=head_col(shift, i),
                                     in1=st[i][b][:, cols], op0=ALU.add, op1=ALU.mult)

        def products_of(i, cols):
            shifted_product(i, "cubic", "square", coef["rho1"], "x", cols)
            shifted_product(i, "mixed", "x", coef["rho"], "w", cols)

        def square_half(i, engine, cols=WHOLE):
            if "w" not in st[i]:
                st[i]["w"] = wide("w_late") if i >= last - 1 else wide("w", bufs=1)
            if engine is act:
                act.activation(out=st[i]["w"][:, cols], in_=st[i]["half"][:, cols], func=ACT.Square)
            else:
                pool_engine.tensor_tensor(out=st[i]["w"][:], in0=st[i]["half"][:], in1=st[i]["half"][:], op=ALU.mult)

        def sum_turned(i, c, tag):
            bank = psum.tile([P, PACK, P], F32, name="sum_bank", tag=tag, bufs=BANKS[tag])
            for t in range(PACK):
                cols = slice((c * PACK + t) * P, (c * PACK + t + 1) * P)
                pe.matmul(out=bank[:, t, :], lhsT=st[i]["mixed"][:, cols], rhs=ident[:], is_transpose=True, start=True, stop=False)
                pe.matmul(out=bank[:, t, :], lhsT=st[i]["cubic"][:, cols], rhs=ident[:], is_transpose=True, start=False, stop=True)
            st[i].setdefault("sum", []).append(bank)

        def gained(i, passes=range(PASSES)):
            h = i // Q_TILES
            if "ag" not in st[i]:
                st[i]["ag"] = wide("ag", BF16)
            ag = st[i]["ag"]
            for c in passes:
                row = h * PASSES + c
                vec.scalar_tensor_tensor(
                    out=ag[:, c * K_PASS:(c + 1) * K_PASS].rearrange("p (r t) -> p r t", t=PACK),
                    in0=st[i]["sum"][c][:].rearrange("p t r -> p r t"), scalar=head_col(coef["kappa"], i),
                    in1=gain_lead[:, row:row + 1, :].to_broadcast([P, P, PACK]), op0=ALU.add, op1=ALU.mult)

        def quantize_ag(i, parts=1):
            codes = work.tile([P, PASSES * P], U32, name="ag_codes", align_bytes=64, bufs=10)
            scales = work.tile([P, PASSES * P], U8, name="ag_scales", align_bytes=64, bufs=10)
            width = PASSES * P // parts
            for j in range(parts):
                cols = slice(j * width, (j + 1) * width)
                quantize(codes[:, cols], scales[:, cols], st[i]["ag"][:, j * width * PACK:(j + 1) * width * PACK])
            st[i]["codes"], st[i]["scales"] = codes, scales

        def mix_values(i, tag="out"):
            h = i // Q_TILES
            bank = psum.tile([P, DV], F32, name="out_bank", tag=tag, bufs=BANKS[tag])
            for c in range(PASSES):
                cols = slice(c * P, (c + 1) * P)
                pe.matmul_mx(out=bank[:], lhsT=st[i]["codes"][:, cols].bitcast(FP8X4), lhsT_scale=st[i]["scales"][:, cols],
                             rhs=v_codes[h][c][:].bitcast(FP8X4), rhs_scale=v_scales[h][c][:], start=(c == 0), stop=(c == PASSES - 1))
            st[i]["out"] = bank

        def store(i):
            h, row = divmod(i, Q_TILES)
            result = work.tile([P, DV], F32, name="result", bufs=3)
            act.activation(out=result[:], in_=st[i]["out"][:], func=ACT.Copy, scale=1.0 / math.sqrt(TK))
            dma.dma_start(out=out[h, row * P:(row + 1) * P, :], in_=result[:])

        loop_jobs = [q_job(3)] + [k_job(1, j) for j in range(2 * PASSES)] + [q_job(j) for j in range(4, TILES // 2)]
        JOB_START = 2
        job_bank = {}
        job_staged = {}
        v_blocks = [(0, 1), (1, 0), (1, 1)]
        v_tiles = {}
        V_START = 4
        V_WIDENS = 1
        V_UNITS = 2 * PACK
        V_STEPS = 10
        CATCH_UP = 13

        def v_unit(n, engine):
            block, unit_index = divmod(n, V_UNITS)
            if (engine is vec) != (unit_index < PACK and block < V_WIDENS):
                return
            h, c = v_blocks[block]
            if unit_index == 0:
                v_tiles[block] = (v_planes_tile(), v_woven_tile())
            planes, woven = v_tiles[block]
            if unit_index < PACK:
                widen_v(h, c, unit_index, planes, engine)
            else:
                part = unit_index - PACK
                interleave_v(planes, woven, slice(part * DV // PACK, (part + 1) * DV // PACK), act)

        def live(i):
            return 0 <= i < TILES

        last = TILES - 1
        waiting = list(range(last))
        def unit_step(n):
            return V_START + n * V_STEPS // (len(v_blocks) * V_UNITS)

        v_done = [unit_step((block + 1) * V_UNITS - 1) + 1 for block in range(len(v_blocks))]

        mixed_tiles = []

        def mix_next(s):
            if waiting and s >= max(waiting[0] + 5, v_done[2 * (waiting[0] // Q_TILES)]):
                mixed_tiles.append(waiting.pop(0))
                mix_values(mixed_tiles[-1], "out")

        def store_next():
            if mixed_tiles:
                store(mixed_tiles.pop(0))

        scores(0, 0)
        whole(0, 0)
        head_quantize(4, staged4)
        rest(0, 0)
        head_quantize(5, staged5)
        scores(0, 1)
        for c in range(PASSES):
            scores(1, c)
        bank_q1 = turn(q_job(1), "sum")
        bank_q2 = turn(q_job(2), "sum")
        coefficients(0)
        whole(0, 1)
        coefficients(1)
        interleave_v(planes0[0], woven0[0], slice(0, DV // 4), vec)
        rest(0, 1)
        for cols in HALVES:
            folded(0, cols)
            half_sine(0, cols)
            sine(0, cols)
            square_half(0, act, cols)
            squared(0, cols)
        coefficients(2)
        whole(1, 0)
        coefficients(3)
        whole(1, 1)
        coefficients(4)
        rest(1, 0)
        staged_q1 = turned_copy(bank_q1, vec)
        coefficients(5)
        rest(1, 1)
        coefficients(6)
        quantize(q_job(1)[1], q_job(1)[2], staged_q1[:])
        interleave_v(planes0[0], woven0[0], slice(DV // 4, DV), vec)
        job_bank[JOB_START] = turn(loop_jobs[0], "turn")
        for c in range(PASSES):
            scores(2, c)
        for s in range(3, TILES + 1):
            folded(s - 2)
            half_sine(s - 2)
            sine(s - 2)
            if s - 1 in job_bank and s != 4:
                job_staged[s - 1] = turned_copy(job_bank[s - 1], act)
            else:
                store_next()
            squared(s - 2)
            if s - 2 == last - 1:
                square_half(s - 2, act)
            store_next()
            for n in range(len(v_blocks) * V_UNITS):
                if unit_step(n) == s:
                    v_unit(n, act)
            if s == 3:
                staged_q2 = turned_copy(bank_q2, vec)
            else:
                products_of(s - 4, WHOLE)
                square_half(s - 3, pool_engine)
            if s == 4:
                job_staged[s - 1] = turned_copy(job_bank[s - 1], vec)
            if s >= 5:
                gained(s - 5)
            for c in range(PASSES):
                whole(s - 1, c)
            for c in range(PASSES):
                rest(s - 1, c)
            if s == 3:
                quantize(v_codes[0][0][:], v_scales[0][0][:], woven0[0][:])
                quantize(q_job(2)[1], q_job(2)[2], staged_q2[:])
            else:
                for c in range(PASSES):
                    sum_turned(s - 4, c, "sum")
            if s >= 5:
                quantize_ag(s - 5)
            if s - 1 in job_staged:
                quantize(loop_jobs[s - 1 - JOB_START][1], loop_jobs[s - 1 - JOB_START][2], job_staged[s - 1][:])
            for block in range(len(v_blocks)):
                if s == v_done[block]:
                    h, c = v_blocks[block]
                    quantize(v_codes[h][c][:], v_scales[h][c][:], v_tiles[block][1][:])
            for n in range(len(v_blocks) * V_UNITS):
                if unit_step(n) == s + 1:
                    v_unit(n, vec)
            if s < TILES:
                for c in range(PASSES):
                    scores(s, c)
            if s - JOB_START < len(loop_jobs):
                job_bank[s] = turn(loop_jobs[s - JOB_START], "turn")
            mix_next(s)
            if s >= CATCH_UP:
                mix_next(s)
        for cols in HALVES:
            folded(last, cols)
            half_sine(last, cols)
            sine(last, cols)
            square_half(last, act, cols)
            squared(last, cols)
        drain_tags = {last - 2: ["score", "score"], last - 1: ["sum", "sum"], last: ["score", "score"]}
        for i in range(last - 2, TILES):
            for c in range(PASSES):
                products_of(i, HALVES[c])
                sum_turned(i, c, drain_tags[i][c])
                if c == 0 and i > last - 2:
                    quantize_ag(i - 2)
            while waiting and waiting[0] <= i - 2:
                store_next()
                mix_next(TILES + 5)
            gained(i - 1)
        gained(last, [0])
        quantize_ag(last - 1)
        gained(last, [1])
        store_next()
        mix_next(TILES + 5)
        quantize_ag(last, PASSES)
        store_next()
        store_next()
        h, row = divmod(last, Q_TILES)
        for part in range(2):
            cols = slice(part * DV // 2, (part + 1) * DV // 2)
            bank = psum.tile([P, DV // 2], F32, name="last_bank", tag="score", bufs=BANKS["score"])
            for c in range(PASSES):
                rows = slice(c * P, (c + 1) * P)
                pe.matmul_mx(out=bank[:], lhsT=st[last]["codes"][:, rows].bitcast(FP8X4), lhsT_scale=st[last]["scales"][:, rows],
                             rhs=v_codes[h][c][:, cols].bitcast(FP8X4), rhs_scale=v_scales[h][c][:, cols], start=(c == 0), stop=(c == PASSES - 1))
            piece = work.tile([P, DV // 2], F32, name="piece")
            if part == 0:
                vec.tensor_scalar(out=piece[:], in0=bank[:], scalar1=1.0 / math.sqrt(TK), scalar2=None, op0=ALU.mult)
                dma.dma_start(out=out[h, row * P:(row + 1) * P, cols], in_=piece[:])
            else:
                act.activation(out=piece[:], in_=bank[:], func=ACT.Copy, scale=1.0 / math.sqrt(TK))
                act.dma_start(out=out[h, row * P:(row + 1) * P, cols], in_=piece[:])
